import numpy as np
import ml_dtypes


def mxq(x, axis, fmt="e4m3"):
    dtype, down = {"e4m3": (ml_dtypes.float8_e4m3fn, 7), "e5m2": (ml_dtypes.float8_e5m2, 14)}[fmt]
    v = np.moveaxis(np.asarray(x, np.float32).astype(ml_dtypes.bfloat16).astype(np.float64), axis, -1)
    blocks = v.reshape(v.shape[:-1] + (-1, 32))
    amax = np.abs(blocks).max(-1, keepdims=True)
    byte = np.maximum(np.where(amax > 0, np.frexp(amax)[1] - 1 + 127, 0) - down, 1)
    scale = np.exp2(byte - 127.0)
    codes = (blocks / scale).astype(np.float32).astype(dtype).astype(np.float64)
    return np.moveaxis((codes * scale).reshape(v.shape), -1, axis)


WIDE = False


def mx_kscale(k):
    if not WIDE:
        return np.ones(k)
    levels = np.array([10, -10, 5, -5, 0])
    if k % 512:
        return np.exp2(np.random.permutation(np.resize(levels, k // 32))).repeat(32)
    a = np.empty((k // 512, 16))
    for p in range(k // 512):
        a[p, :8] = np.random.permutation(np.resize(levels, 8))
        for g in range(8):
            far = levels[np.abs(levels - a[p, g]) >= 10]
            a[p, g + 8] = far[np.random.randint(len(far))]
    return np.exp2(a.ravel()).repeat(32)


def f64(x):
    return np.asarray(x).astype(np.float64)


def striped(idx):
    return np.tile(idx.reshape(-1, 16).T, (8, 1)).astype(np.uint16)


def unstriped(offs):
    return offs[:16].T.reshape(-1).astype(np.int64)


def pack_weight(w):
    k, n = w.shape
    w = f64(np.asarray(w, np.float32).astype(ml_dtypes.bfloat16)).reshape(k // 32, 32, n)
    amax = np.abs(w).max(1)
    byte = np.clip(np.where(amax > 0, np.frexp(amax)[1] - 1 + 127 - 7, 1), 1, 254)
    scaled = (w * np.exp2(127.0 - byte)[:, None, :]).reshape(k, n).astype(np.float32)
    words = np.ascontiguousarray(scaled.reshape(k // 512, 128, 4, n).transpose(0, 1, 3, 2)).astype(ml_dtypes.float8_e4m3fn).view(np.uint8)
    return words, np.ascontiguousarray(byte.astype(np.uint8).reshape(k // 512, 16, n))


def unpack_weight(words, scales):
    g, p, n, _ = words.shape
    vals = np.ascontiguousarray(words).view(ml_dtypes.float8_e4m3fn).astype(np.float64) * np.repeat(np.exp2(scales.astype(np.float64) - 127.0), 8, axis=1)[..., None]
    return vals.transpose(0, 1, 3, 2).reshape(g * 512, n)


def relu(v):
    return np.maximum(v, 0.0)


K, T, H, N = 1024, 512, 512, 256


def setup_inputs():
    n = np.random.standard_normal
    s = mx_kscale(K)[:, None]
    u = mx_kscale(H)
    packed_xT = pack_weight(n((K, T)) * s)
    return {
        "x_words": packed_xT[0],
        "x_scales": packed_xT[1],
        "w1": (n((K, H)) / np.sqrt(K) / s * u).astype(np.float32),
        "w2": (n((H, N)) / np.sqrt(2 * H) / u[:, None]).astype(np.float32),
        "w3": (n((H, N)) / np.sqrt(2 * H) / u[:, None]).astype(np.float32),
        "pos1": striped(np.random.permutation(T)),
        "pos2": striped(np.random.permutation(T)),
        "pos3": striped(np.random.permutation(T)),
    }


def reference(x_words, x_scales, w1, w2, w3, pos1, pos2, pos3):
    xq = unpack_weight(x_words, x_scales)
    h = relu(mxq(f64(w1), 0, "e4m3").T @ xq)
    z = np.maximum(np.maximum(h[:, unstriped(pos1)], h[:, unstriped(pos2)]), h[:, unstriped(pos3)])
    return relu(mxq(f64(w2), 0, "e4m3").T @ mxq(h, 0, "e4m3") + mxq(f64(w3), 0, "e4m3").T @ mxq(z, 0, "e4m3"))

@@ -1,0 +1,240 @@
+from contextlib import ExitStack
+
+import concourse.mybir as mybir
+
+K, T, H, N = 1024, 512, 512, 256
+FLOPS = 2 * K * H * T + 2 * 2 * H * N * T
+
+F32 = mybir.dt.float32
+BF16 = mybir.dt.bfloat16
+I32 = mybir.dt.int32
+U32 = mybir.dt.uint32
+U16 = mybir.dt.uint16
+U8 = mybir.dt.uint8
+FP8X4 = mybir.dt.float8_e4m3fn_x4
+RELU = mybir.ActivationFunctionType.Relu
+COPY = mybir.ActivationFunctionType.Copy
+MAX = mybir.AluOpType.max
+
+P = 128
+PACK = 4
+K_PASS = P * PACK
+PASSES = K // K_PASS
+RUN = 8
+HALF = T // 2
+FIRST = 384
+LAST = T - FIRST
+ALIGN = 64
+
+
+def tile_picked_wsagecat_maxrelu_l_kernel(
+    tc, x_words, x_scales, w1, w2, w3, pos1, pos2, pos3, out
+):
+    nc = tc.nc
+    with ExitStack() as ctx:
+        lists = ctx.enter_context(tc.tile_pool(name="lists", bufs=1))
+        sb = ctx.enter_context(tc.tile_pool(name="sb", bufs=1))
+        ps = ctx.enter_context(tc.psum_pool(name="ps", bufs=1))
+
+        def tile(name, shape, dtype, tag=None):
+            return sb.tile(shape, dtype, name=name, tag=tag or name, align_bytes=ALIGN)
+
+        def quantize(codes, scales, values):
+            nc.vector.quantize_mx(out=codes.bitcast(FP8X4), scales=scales, in_=values)
+
+        def mx(acc, lhs_codes, lhs_scales, rhs_codes, rhs_scales, start, stop):
+            nc.tensor.matmul_mx(
+                out=acc,
+                lhsT=lhs_codes.bitcast(FP8X4),
+                lhsT_scale=lhs_scales,
+                rhs=rhs_codes.bitcast(FP8X4),
+                rhs_scale=rhs_scales,
+                start=start,
+                stop=stop,
+            )
+
+        planes = tile("planes", [P, T], U8)
+        w1_raw = [tile("w1_raw%d" % g, [P, PACK, H], F32) for g in range(PASSES)]
+        for g in range(PASSES):
+            nc.sync.dma_start(
+                out=w1_raw[g][:],
+                in_=w1[g * K_PASS : (g + 1) * K_PASS, :].rearrange("(p j) c -> p j c", j=PACK),
+            )
+            if g == 0:
+                for q in range(4):
+                    nc.sync.dma_start(
+                        out=planes[32 * q + 4 : 32 * q + 4 + 4 * PASSES, :].bitcast(I32),
+                        in_=x_scales[:, 4 * q : 4 * q + 4, :].bitcast(I32),
+                    )
+        x_codes = [tile("x_codes%d" % g, [P, T], U32) for g in range(PASSES)]
+        for g, c0, c1 in ((0, 0, T), (1, 0, HALF), (1, HALF, T)):
+            nc.sync.dma_start(
+                out=x_codes[g][:, c0:c1].bitcast(I32),
+                in_=x_words[g].rearrange("p n t -> p (n t)")[:, c0 * PACK : c1 * PACK].bitcast(I32),
+            )
+        offs = []
+        for d, pos in enumerate((pos1, pos2, pos3)):
+            lst = lists.tile([P, T // 16], U16, name="list%d" % d, tag="list%d" % d)
+            nc.sync.dma_start(lst[:], pos)
+            offs.append(lst)
+
+        w1_bf = {}
+        w1_codes = {}
+        w1_scales = {}
+        for g in range(PASSES):
+            for t in range(PACK):
+                w1_bf[g, t] = tile("w1_bf%d%d" % (g, t), [P, K_PASS], BF16)
+                w1_codes[g, t] = tile("w1_codes%d%d" % (g, t), [P, P], U32)
+                if g == 0:
+                    w1_scales[g, t] = planes[:, t * P : (t + 1) * P]
+                else:
+                    w1_scales[g, t] = tile("w1_scales%d%d" % (g, t), [P, P], U8)[:]
+
+        def round_w1(g, t, on_vector, b0=0, b1=16):
+            src = w1_raw[g][:].rearrange("p j (b t r) -> p t b r j", t=PACK, r=RUN)[:, t, b0:b1]
+            dst = w1_bf[g, t][:].rearrange("p (b r j) -> p b r j", r=RUN, j=PACK)[:, b0:b1]
+            if on_vector:
+                nc.vector.tensor_copy(out=dst, in_=src)
+            else:
+                nc.scalar.activation(out=dst, in_=src, func=COPY)
+
+        def quantize_w1(g, t):
+            quantize(w1_codes[g, t][:], w1_scales[g, t], w1_bf[g, t][:])
+
+        for t in range(PACK):
+            round_w1(0, t, t < 2)
+        for t in range(PACK):
+            quantize_w1(0, t)
+        round_w1(1, 0, True, 0, 10)
+        round_w1(1, 0, False, 10, 16)
+        quantize_w1(1, 0)
+        round_w1(1, 1, True)
+        round_w1(1, 2, False)
+        round_w1(1, 3, True)
+        for t in range(1, PACK):
+            quantize_w1(1, t)
+
+        w23_raw = tile("w23_raw", [P, 2, PACK, N], F32, tag="w1_raw0")
+        for s, w in enumerate((w2, w3)):
+            for t in range(PACK):
+                nc.sync.dma_start(
+                    out=w23_raw[:, s, t, :],
+                    in_=w.rearrange("(b t r) n -> t b r n", t=PACK, r=RUN)[t],
+                )
+
+        h = tile("h", [P, PACK * T], F32)
+        for t in range(PACK):
+            pieces = [(0, HALF), (HALF, T)] if t == 0 else [(0, T)]
+            for c0, c1 in pieces:
+                acc = ps.tile([P, c1 - c0], F32, name="h_acc%d_%d" % (t, c0), tag="h_acc%d_%d" % (t, c0))
+                order = (0, 1) if t == 0 else (1, 0)
+                for g in order:
+                    mx(acc[:], w1_codes[g, t][:], w1_scales[g, t],
+                       x_codes[g][:, c0:c1], planes[4 + 4 * g : P, c0:c1], g == order[0], g == order[1])
+                nc.scalar.activation(out=h[:, t * T + c0 : t * T + c1], in_=acc[:], func=RELU)
+
+        h_bf = tile("h_bf", [P, T * PACK], BF16)
+        nc.scalar.copy(out=h_bf[:].rearrange("p (v t) -> p v t", t=PACK),
+                       in_=h[:].rearrange("p (t v) -> p v t", t=PACK))
+        w23_bf = tile("w23_bf", [P, 2, N * PACK], BF16)
+        for s in range(2):
+            nc.scalar.copy(out=w23_bf[:, s, :].rearrange("p (n t) -> p n t", t=PACK),
+                           in_=w23_raw[:, s].rearrange("p t n -> p n t"))
+
+        def gather(dst, t, d, v0, v1):
+            window = h[:, t * T : (t + 1) * T]
+            nc.vector.tensor_copy(out=dst, in_=window.indirect(offs[d][:, v0 // 16 : v1 // 16]))
+
+        blocks = FIRST // P
+        a0 = tile("a0", [P, blocks, PACK, P], BF16)
+        a1 = [tile("a1_0", [P, blocks, 2, P], BF16)]
+        a2 = [tile("a2_0", [P, blocks, 2, P], BF16)]
+        h_codes = tile("h_codes", [P, T], U32)
+        h_scales = tile("h_scales", [P, T], U8)
+        w23_codes = tile("w23_codes", [P, 2 * N], U32)
+        w23_scales = tile("w23_scales", [P, 2 * N], U8)
+
+        def gather_first(t, d):
+            dst = a0[:, :, t, :] if d == 0 else (a1, a2)[d - 1][t // 2][:, :, t % 2, :]
+            gather(dst, t, d, 0, FIRST)
+
+        def max_first(u, other):
+            pair = a0[:, :, 2 * u : 2 * u + 2, :]
+            nc.vector.tensor_tensor(out=pair, in0=pair, in1=other[u][:], op=MAX)
+
+        for t in range(2):
+            for d in range(3):
+                gather_first(t, d)
+        max_first(0, a1)
+        gather_first(2, 0)
+        max_first(0, a2)
+        quantize(h_codes[:], h_scales[:], h_bf[:])
+        gather_first(3, 0)
+        a1.append(tile("a1_1", [P, blocks, 2, P], BF16, tag="h_bf"))
+        gather_first(2, 1)
+        quantize(w23_codes[:], w23_scales[:], w23_bf[:].rearrange("p s c -> p (s c)"))
+        gather_first(3, 1)
+        a2.append(tile("a2_1", [P, blocks, 2, P], BF16, tag="w23_bf"))
+        gather_first(2, 2)
+        max_first(1, a1)
+        gather_first(3, 2)
+
+        def weights(s, m):
+            cols = slice(s * N + m * P, s * N + (m + 1) * P)
+            return w23_codes[:, cols], w23_scales[:, cols]
+
+        groups = [(0, HALF), (HALF, FIRST), (FIRST, T)]
+        banks = ["h_acc0_0", "h_acc0_%d" % HALF, "h_acc1_0", "h_acc2_0", "h_acc3_0", "out_acc"]
+        out_acc = {}
+        for i, (c0, c1) in enumerate(groups):
+            for m in range(N // P):
+                acc = ps.tile([P, c1 - c0], F32, name="out_acc%d%d" % (i, m), tag=banks[2 * i + m])
+                mx(acc[:], *weights(0, m), h_codes[:, c0:c1], h_scales[:, c0:c1], True, False)
+                out_acc[i, m] = acc
+
+        run = LAST // 2
+        b0 = tile("b0", [P, 2, PACK, run], BF16, tag="h_bf")
+        gather(b0[:, :, 0, :], 0, 0, FIRST, T)
+        max_first(1, a2)
+        za_bf = tile("za_bf", [P, FIRST * PACK], BF16)
+        nc.scalar.copy(out=za_bf[:].rearrange("p (b v t) -> p b v t", v=P, t=PACK),
+                       in_=a0[:].rearrange("p b t v -> p b v t"))
+        for t in range(1, PACK):
+            gather(b0[:, :, t, :], t, 0, FIRST, T)
+        b1 = tile("b1", [P, 2, PACK, run], BF16, tag="w23_bf")
+        for t in range(PACK):
+            gather(b1[:, :, t, :], t, 1, FIRST, T)
+
+        za_codes = tile("za_codes", [P, FIRST], U32)
+        za_scales = tile("za_scales", [P, FIRST], U8)
+        for c0, c1 in groups[:2]:
+            quantize(za_codes[:, c0:c1], za_scales[:, c0:c1], za_bf[:, c0 * PACK : c1 * PACK])
+        nc.vector.tensor_tensor(out=b0[:], in0=b0[:], in1=b1[:], op=MAX)
+
+        for m in range(N // P):
+            res = tile("first_out%d" % m, [P, FIRST], F32)
+            for i, (c0, c1) in enumerate(groups[:2]):
+                acc = out_acc[i, m]
+                mx(acc[:], *weights(1, m), za_codes[:, c0:c1], za_scales[:, c0:c1], False, True)
+                nc.scalar.activation(out=res[:, c0:c1], in_=acc[:], func=RELU)
+            nc.sync.dma_start(out=out[m * P : (m + 1) * P, 0:FIRST], in_=res[:])
+
+        b2 = tile("b2", [P, 2, PACK, run], BF16, tag="za_bf")
+        for t in range(PACK):
+            gather(b2[:, :, t, :], t, 2, FIRST, T)
+        zb_bf = tile("zb_bf", [P, LAST * PACK], BF16)
+        nc.vector.tensor_tensor(
+            out=zb_bf[:].rearrange("p (b v t) -> p b v t", v=run, t=PACK),
+            in0=b0[:].rearrange("p b t v -> p b v t"),
+            in1=b2[:].rearrange("p b t v -> p b v t"),
+            op=MAX,
+        )
+        zb_codes = tile("zb_codes", [P, LAST], U32)
+        zb_scales = tile("zb_scales", [P, LAST], U8)
+        quantize(zb_codes[:], zb_scales[:], zb_bf[:])
+        res = tile("last_out", [P, N // P, LAST], F32)
+        for m in range(N // P):
+            mx(out_acc[2, m][:], *weights(1, m), zb_codes[:], zb_scales[:], False, True)
+        nc.scalar.activation(out=res[:, 0, :], in_=out_acc[2, 0][:], func=RELU)
+        nc.vector.tensor_scalar(out=res[:, 1, :], in0=out_acc[2, 1][:], scalar1=0.0, scalar2=None, op0=MAX)
+        nc.sync.dma_start(out=out[:, FIRST:T].rearrange("(m p) v -> p m v", p=P), in_=res[:])

@@ -83,34 +83,40 @@ def tile_picked_wsagecat_maxrelu_l_kernel(
         w1_scales = {}
         for g in range(PASSES):
             for t in range(PACK):
-                w1_bf[g, t] = tile("w1_bf%d%d" % (g, t), [P, K_PASS], BF16)
                 w1_codes[g, t] = tile("w1_codes%d%d" % (g, t), [P, P], U32)
                 if g == 0:
                     w1_scales[g, t] = planes[:, t * P : (t + 1) * P]
                 else:
                     w1_scales[g, t] = tile("w1_scales%d%d" % (g, t), [P, P], U8)[:]
 
-        def round_w1(g, t, on_vector, b0=0, b1=16):
-            src = w1_raw[g][:].rearrange("p j (b t r) -> p t b r j", t=PACK, r=RUN)[:, t, b0:b1]
-            dst = w1_bf[g, t][:].rearrange("p (b r j) -> p b r j", r=RUN, j=PACK)[:, b0:b1]
-            if on_vector:
+        def round_w1(g, t, engine, tag=None, b0=0, b1=16):
+            if b0 == 0:
+                w1_bf[g, t] = tile("w1_bf%d%d" % (g, t), [P, K_PASS], BF16, tag=tag)
+            src = w1_raw[g][:].rearrange("p j (b t c i) -> p t b c j i", t=PACK, c=2, i=4)[:, t, b0:b1]
+            dst = w1_bf[g, t][:].rearrange("p (b c i j) -> p b c j i", c=2, i=4, j=PACK)[:, b0:b1]
+            if engine == "vector":
                 nc.vector.tensor_copy(out=dst, in_=src)
+            elif engine == "scalar":
+                nc.scalar.copy(out=dst, in_=src)
             else:
-                nc.scalar.activation(out=dst, in_=src, func=COPY)
+                nc.scalar.activation(
+                    out=w1_bf[g, t][:].rearrange("p (b r j) -> p b r j", r=RUN, j=PACK),
+                    in_=w1_raw[g][:].rearrange("p j (b t r) -> p t b r j", t=PACK, r=RUN)[:, t],
+                    func=COPY)
 
         def quantize_w1(g, t):
             quantize(w1_codes[g, t][:], w1_scales[g, t], w1_bf[g, t][:])
 
-        for t in range(PACK):
-            round_w1(0, t, t < 2)
+        for t, engine in enumerate(("vector", "vector", "activation", "scalar")):
+            round_w1(0, t, engine)
         for t in range(PACK):
             quantize_w1(0, t)
-        round_w1(1, 0, True, 0, 10)
-        round_w1(1, 0, False, 10, 16)
+        round_w1(1, 0, "vector", None, 0, 10)
+        round_w1(1, 0, "scalar", None, 10, 16)
         quantize_w1(1, 0)
-        round_w1(1, 1, True)
-        round_w1(1, 2, False)
-        round_w1(1, 3, True)
+        round_w1(1, 1, "scalar")
+        round_w1(1, 2, "scalar")
+        round_w1(1, 3, "vector", tag="w1_bf10")
         for t in range(1, PACK):
             quantize_w1(1, t)
 
@@ -134,12 +140,12 @@ def tile_picked_wsagecat_maxrelu_l_kernel(
                 nc.scalar.activation(out=h[:, t * T + c0 : t * T + c1], in_=acc[:], func=RELU)
 
         h_bf = tile("h_bf", [P, T * PACK], BF16)
-        nc.scalar.copy(out=h_bf[:].rearrange("p (v t) -> p v t", t=PACK),
-                       in_=h[:].rearrange("p (t v) -> p v t", t=PACK))
+        nc.scalar.copy(out=h_bf[:].rearrange("p (c i t) -> p c t i", i=4, t=PACK),
+                       in_=h[:].rearrange("p (t c i) -> p c t i", t=PACK, i=4))
         w23_bf = tile("w23_bf", [P, 2, N * PACK], BF16)
         for s in range(2):
-            nc.scalar.copy(out=w23_bf[:, s, :].rearrange("p (n t) -> p n t", t=PACK),
-                           in_=w23_raw[:, s].rearrange("p t n -> p n t"))
+            nc.scalar.copy(out=w23_bf[:, s, :].rearrange("p (c i t) -> p c t i", i=4, t=PACK),
+                           in_=w23_raw[:, s].rearrange("p t (c i) -> p c t i", i=4))
 
         def gather(dst, t, d, v0, v1):
             window = h[:, t * T : (t + 1) * T]
@@ -197,8 +203,8 @@ def tile_picked_wsagecat_maxrelu_l_kernel(
         gather(b0[:, :, 0, :], 0, 0, FIRST, T)
         max_first(1, a2)
         za_bf = tile("za_bf", [P, FIRST * PACK], BF16)
-        nc.scalar.copy(out=za_bf[:].rearrange("p (b v t) -> p b v t", v=P, t=PACK),
-                       in_=a0[:].rearrange("p b t v -> p b v t"))
+        nc.scalar.copy(out=za_bf[:].rearrange("p (b c i t) -> p b c t i", b=blocks, i=4, t=PACK),
+                       in_=a0[:].rearrange("p b t (c i) -> p b c t i", i=4))
         for t in range(1, PACK):
             gather(b0[:, :, t, :], t, 0, FIRST, T)
         b1 = tile("b1", [P, 2, PACK, run], BF16, tag="w23_bf")
@@ -220,18 +226,24 @@ def tile_picked_wsagecat_maxrelu_l_kernel(
             nc.sync.dma_start(out=out[m * P : (m + 1) * P, 0:FIRST], in_=res[:])
 
         b2 = tile("b2", [P, 2, PACK, run], BF16, tag="za_bf")
-        for t in range(PACK):
+
+        def max_last(t0, t1):
+            nc.vector.tensor_tensor(out=b0[:, :, t0:t1, :], in0=b0[:, :, t0:t1, :], in1=b2[:, :, t0:t1, :], op=MAX)
+
+        for t in range(PACK - 1):
             gather(b2[:, :, t, :], t, 2, FIRST, T)
-        zb_bf = tile("zb_bf", [P, LAST * PACK], BF16)
-        nc.vector.tensor_tensor(
-            out=zb_bf[:].rearrange("p (b v t) -> p b v t", v=run, t=PACK),
-            in0=b0[:].rearrange("p b t v -> p b v t"),
-            in1=b2[:].rearrange("p b t v -> p b v t"),
-            op=MAX,
-        )
+        max_last(0, 2)
+        gather(b2[:, :, PACK - 1, :], PACK - 1, 2, FIRST, T)
+        max_last(2, 3)
+        max_last(3, 4)
+        zb_bf = tile("zb_bf", [P, 2, run * PACK], BF16)
+        for b in range(2):
+            nc.vector.tensor_copy(out=zb_bf[:, b, :].rearrange("p (c i t) -> p c t i", i=4, t=PACK),
+                                  in_=b0[:, b].rearrange("p t (c i) -> p c t i", i=4))
         zb_codes = tile("zb_codes", [P, LAST], U32)
         zb_scales = tile("zb_scales", [P, LAST], U8)
-        quantize(zb_codes[:], zb_scales[:], zb_bf[:])
+        for b in range(2):
+            quantize(zb_codes[:, b * run : (b + 1) * run], zb_scales[:, b * run : (b + 1) * run], zb_bf[:, b, :])
         res = tile("last_out", [P, N // P, LAST], F32)
         for m in range(N // P):
             mx(out_acc[2, m][:], *weights(1, m), zb_codes[:], zb_scales[:], False, True)

@@ -25,6 +25,9 @@ HALF = T // 2
 FIRST = 384
 LAST = T - FIRST
 ALIGN = 64
+ORDER = (3, 2, 1, 0)
+SPARE = 192
+BLOCK = 64
 
 
 def tile_picked_wsagecat_maxrelu_l_kernel(
@@ -55,23 +58,30 @@ def tile_picked_wsagecat_maxrelu_l_kernel(
 
         planes = tile("planes", [P, T], U8)
         w1_raw = [tile("w1_raw%d" % g, [P, PACK, H], F32) for g in range(PASSES)]
-        for g in range(PASSES):
+        x_codes = [tile("x_codes%d" % g, [P, T], U32) for g in range(PASSES)]
+
+        def load_w1(g):
             nc.sync.dma_start(
                 out=w1_raw[g][:],
                 in_=w1[g * K_PASS : (g + 1) * K_PASS, :].rearrange("(p j) c -> p j c", j=PACK),
             )
-            if g == 0:
-                for q in range(4):
-                    nc.sync.dma_start(
-                        out=planes[32 * q + 4 : 32 * q + 4 + 4 * PASSES, :].bitcast(I32),
-                        in_=x_scales[:, 4 * q : 4 * q + 4, :].bitcast(I32),
-                    )
-        x_codes = [tile("x_codes%d" % g, [P, T], U32) for g in range(PASSES)]
-        for g, c0, c1 in ((0, 0, T), (1, 0, HALF), (1, HALF, T)):
+
+        def load_x(g, c0, c1):
             nc.sync.dma_start(
                 out=x_codes[g][:, c0:c1].bitcast(I32),
                 in_=x_words[g].rearrange("p n t -> p (n t)")[:, c0 * PACK : c1 * PACK].bitcast(I32),
             )
+
+        load_w1(0)
+        for q in range(4):
+            nc.sync.dma_start(
+                out=planes[32 * q + 4 : 32 * q + 4 + 4 * PASSES, :].bitcast(I32),
+                in_=x_scales[:, 4 * q : 4 * q + 4, :].bitcast(I32),
+            )
+        load_x(0, 0, T)
+        load_w1(1)
+        load_x(1, 0, HALF)
+        load_x(1, HALF, T)
         offs = []
         for d, pos in enumerate((pos1, pos2, pos3)):
             lst = lists.tile([P, T // 16], U16, name="list%d" % d, tag="list%d" % d)
@@ -107,18 +117,19 @@ def tile_picked_wsagecat_maxrelu_l_kernel(
         def quantize_w1(g, t):
             quantize(w1_codes[g, t][:], w1_scales[g, t], w1_bf[g, t][:])
 
-        for t, engine in enumerate(("vector", "vector", "activation", "scalar")):
+        for t, engine in zip(ORDER, ("vector", "vector", "activation", "scalar")):
             round_w1(0, t, engine)
-        for t in range(PACK):
+        for t in ORDER:
             quantize_w1(0, t)
-        round_w1(1, 0, "vector", None, 0, 10)
-        round_w1(1, 0, "scalar", None, 10, 16)
-        quantize_w1(1, 0)
-        round_w1(1, 1, "scalar")
+        round_w1(1, 3, "vector", None, 0, 10)
+        round_w1(1, 3, "scalar", None, 10, 16)
+        quantize_w1(1, 3)
         round_w1(1, 2, "scalar")
-        round_w1(1, 3, "vector", tag="w1_bf10")
-        for t in range(1, PACK):
-            quantize_w1(1, t)
+        round_w1(1, 1, "vector", tag="w1_bf13")
+        quantize_w1(1, 2)
+        quantize_w1(1, 1)
+        round_w1(1, 0, "scalar", tag="w1_bf12")
+        quantize_w1(1, 0)
 
         w23_raw = tile("w23_raw", [P, 2, PACK, N], F32, tag="w1_raw0")
         for s, w in enumerate((w2, w3)):
@@ -128,94 +139,98 @@ def tile_picked_wsagecat_maxrelu_l_kernel(
                     in_=w.rearrange("(b t r) n -> t b r n", t=PACK, r=RUN)[t],
                 )
 
-        h = tile("h", [P, PACK * T], F32)
-        for t in range(PACK):
-            pieces = [(0, HALF), (HALF, T)] if t == 0 else [(0, T)]
-            for c0, c1 in pieces:
-                acc = ps.tile([P, c1 - c0], F32, name="h_acc%d_%d" % (t, c0), tag="h_acc%d_%d" % (t, c0))
-                order = (0, 1) if t == 0 else (1, 0)
-                for g in order:
-                    mx(acc[:], w1_codes[g, t][:], w1_scales[g, t],
-                       x_codes[g][:, c0:c1], planes[4 + 4 * g : P, c0:c1], g == order[0], g == order[1])
-                nc.scalar.activation(out=h[:, t * T + c0 : t * T + c1], in_=acc[:], func=RELU)
+        h = tile("h", [P, PACK * T + SPARE], F32)
+        nc.gpsimd.memset(h[:, PACK * T :], 0.0)
+        h_groups = [(ORDER[0], 0, HALF), (ORDER[0], HALF, T)] + [(t, 0, T) for t in ORDER[1:]]
+        h_acc = [ps.tile([P, c1 - c0], F32, name="h_acc%d" % i, tag="bank%d" % i)
+                 for i, (t, c0, c1) in enumerate(h_groups)]
+        for g in range(PASSES):
+            for acc, (t, c0, c1) in zip(h_acc, h_groups):
+                mx(acc[:], w1_codes[g, t][:], w1_scales[g, t],
+                   x_codes[g][:, c0:c1], planes[4 + 4 * g : P, c0:c1], g == 0, g == PASSES - 1)
+                if g == PASSES - 1 and c0 == HALF:
+                    nc.vector.tensor_scalar(out=h[:, t * T + c0 : t * T + c1], in0=acc[:], scalar1=0.0, scalar2=None, op0=MAX)
+                elif g == PASSES - 1:
+                    nc.scalar.activation(out=h[:, t * T + c0 : t * T + c1], in_=acc[:], func=RELU)
 
         h_bf = tile("h_bf", [P, T * PACK], BF16)
         nc.scalar.copy(out=h_bf[:].rearrange("p (c i t) -> p c t i", i=4, t=PACK),
-                       in_=h[:].rearrange("p (t c i) -> p c t i", t=PACK, i=4))
+                       in_=h[:, 0 : PACK * T].rearrange("p (t c i) -> p c t i", t=PACK, i=4))
         w23_bf = tile("w23_bf", [P, 2, N * PACK], BF16)
         for s in range(2):
             nc.scalar.copy(out=w23_bf[:, s, :].rearrange("p (c i t) -> p c t i", i=4, t=PACK),
                            in_=w23_raw[:, s].rearrange("p t (c i) -> p c t i", i=4))
 
         def gather(dst, t, d, v0, v1):
-            window = h[:, t * T : (t + 1) * T]
+            width = T + SPARE if v1 - v0 == T else T
+            window = h[:, t * T : t * T + width]
             nc.vector.tensor_copy(out=dst, in_=window.indirect(offs[d][:, v0 // 16 : v1 // 16]))
 
-        blocks = FIRST // P
-        a0 = tile("a0", [P, blocks, PACK, P], BF16)
-        a1 = [tile("a1_0", [P, blocks, 2, P], BF16)]
-        a2 = [tile("a2_0", [P, blocks, 2, P], BF16)]
+        def vmax(dst, one, other):
+            nc.vector.tensor_tensor(out=dst, in0=one, in1=other, op=MAX)
+
+        nb = T // BLOCK
+        na = FIRST // BLOCK
         h_codes = tile("h_codes", [P, T], U32)
         h_scales = tile("h_scales", [P, T], U8)
         w23_codes = tile("w23_codes", [P, 2 * N], U32)
         w23_scales = tile("w23_scales", [P, 2 * N], U8)
+        za_bf = tile("za_bf", [P, FIRST * PACK], BF16)
+        zb_bf = tile("zb_bf", [P, LAST * PACK], BF16)
 
-        def gather_first(t, d):
-            dst = a0[:, :, t, :] if d == 0 else (a1, a2)[d - 1][t // 2][:, :, t % 2, :]
-            gather(dst, t, d, 0, FIRST)
+        def weave(copy, dst, t0, pair):
+            copy(out=dst.rearrange("p (b c i t) -> p b c t i", c=BLOCK // 4, i=4, t=PACK)[:, :, :, t0 : t0 + 2, :],
+                 in_=pair.rearrange("p b t (c i) -> p b c t i", i=4))
 
-        def max_first(u, other):
-            pair = a0[:, :, 2 * u : 2 * u + 2, :]
-            nc.vector.tensor_tensor(out=pair, in0=pair, in1=other[u][:], op=MAX)
-
-        for t in range(2):
+        e = [tile("e%d" % d, [P, nb, 2, BLOCK], BF16) for d in range(3)]
+        a0 = tile("a0", [P, na, 2, BLOCK], BF16)
+        for t in (3, 2):
             for d in range(3):
-                gather_first(t, d)
-        max_first(0, a1)
-        gather_first(2, 0)
-        max_first(0, a2)
+                gather(e[d][:, :, t - 2, :], t, d, 0, T)
+        vmax(e[0][:], e[0][:], e[1][:])
+        gather(a0[:, :, 1, :], 1, 0, 0, FIRST)
+        vmax(e[0][:], e[0][:], e[2][:])
+        weave(nc.scalar.copy, za_bf[:], 2, e[0][:, 0:na])
+        weave(nc.scalar.copy, zb_bf[:], 2, e[0][:, na:nb])
+
+        gather(a0[:, :, 0, :], 0, 0, 0, FIRST)
         quantize(h_codes[:], h_scales[:], h_bf[:])
-        gather_first(3, 0)
-        a1.append(tile("a1_1", [P, blocks, 2, P], BF16, tag="h_bf"))
-        gather_first(2, 1)
+        a2 = tile("a2", [P, na, 2, BLOCK], BF16)
+        for t in (1, 0):
+            gather(a2[:, :, t, :], t, 2, 0, FIRST)
         quantize(w23_codes[:], w23_scales[:], w23_bf[:].rearrange("p s c -> p (s c)"))
-        gather_first(3, 1)
-        a2.append(tile("a2_1", [P, blocks, 2, P], BF16, tag="w23_bf"))
-        gather_first(2, 2)
-        max_first(1, a1)
-        gather_first(3, 2)
+        vmax(a0[:], a0[:], a2[:])
+        a1 = tile("a1", [P, na, 2, BLOCK], BF16, tag="w23_bf")
+        for t in (1, 0):
+            gather(a1[:, :, t, :], t, 1, 0, FIRST)
+        for t in (1, 0):
+            vmax(a0[:, :, t, :], a0[:, :, t, :], a1[:, :, t, :])
+        weave(nc.scalar.copy, za_bf[:], 0, a0[:])
 
         def weights(s, m):
             cols = slice(s * N + m * P, s * N + (m + 1) * P)
             return w23_codes[:, cols], w23_scales[:, cols]
 
         groups = [(0, HALF), (HALF, FIRST), (FIRST, T)]
-        banks = ["h_acc0_0", "h_acc0_%d" % HALF, "h_acc1_0", "h_acc2_0", "h_acc3_0", "out_acc"]
         out_acc = {}
         for i, (c0, c1) in enumerate(groups):
             for m in range(N // P):
-                acc = ps.tile([P, c1 - c0], F32, name="out_acc%d%d" % (i, m), tag=banks[2 * i + m])
+                acc = ps.tile([P, c1 - c0], F32, name="out_acc%d%d" % (i, m), tag="bank%d" % (2 * i + m))
                 mx(acc[:], *weights(0, m), h_codes[:, c0:c1], h_scales[:, c0:c1], True, False)
                 out_acc[i, m] = acc
 
-        run = LAST // 2
-        b0 = tile("b0", [P, 2, PACK, run], BF16, tag="h_bf")
-        gather(b0[:, :, 0, :], 0, 0, FIRST, T)
-        max_first(1, a2)
-        za_bf = tile("za_bf", [P, FIRST * PACK], BF16)
-        nc.scalar.copy(out=za_bf[:].rearrange("p (b c i t) -> p b c t i", b=blocks, i=4, t=PACK),
-                       in_=a0[:].rearrange("p b t (c i) -> p b c t i", i=4))
-        for t in range(1, PACK):
-            gather(b0[:, :, t, :], t, 0, FIRST, T)
-        b1 = tile("b1", [P, 2, PACK, run], BF16, tag="w23_bf")
-        for t in range(PACK):
-            gather(b1[:, :, t, :], t, 1, FIRST, T)
+        run = BLOCK
+        b01 = tile("b01", [P, 2, 2, 2, BLOCK], BF16, tag="w23_bf")
+        b0 = b01[:, 0]
+        for d in range(2):
+            for t in (1, 0):
+                gather(b01[:, d, :, t, :], t, d, FIRST, T)
+        vmax(b0, b0, b01[:, 1])
 
         za_codes = tile("za_codes", [P, FIRST], U32)
         za_scales = tile("za_scales", [P, FIRST], U8)
         for c0, c1 in groups[:2]:
             quantize(za_codes[:, c0:c1], za_scales[:, c0:c1], za_bf[:, c0 * PACK : c1 * PACK])
-        nc.vector.tensor_tensor(out=b0[:], in0=b0[:], in1=b1[:], op=MAX)
 
         for m in range(N // P):
             res = tile("first_out%d" % m, [P, FIRST], F32)
@@ -225,25 +240,17 @@ def tile_picked_wsagecat_maxrelu_l_kernel(
                 nc.scalar.activation(out=res[:, c0:c1], in_=acc[:], func=RELU)
             nc.sync.dma_start(out=out[m * P : (m + 1) * P, 0:FIRST], in_=res[:])
 
-        b2 = tile("b2", [P, 2, PACK, run], BF16, tag="za_bf")
-
-        def max_last(t0, t1):
-            nc.vector.tensor_tensor(out=b0[:, :, t0:t1, :], in0=b0[:, :, t0:t1, :], in1=b2[:, :, t0:t1, :], op=MAX)
-
-        for t in range(PACK - 1):
+        b2 = tile("b2", [P, 2, 2, BLOCK], BF16, tag="za_bf")
+        for t in (1, 0):
             gather(b2[:, :, t, :], t, 2, FIRST, T)
-        max_last(0, 2)
-        gather(b2[:, :, PACK - 1, :], PACK - 1, 2, FIRST, T)
-        max_last(2, 3)
-        max_last(3, 4)
-        zb_bf = tile("zb_bf", [P, 2, run * PACK], BF16)
+        for t in (1, 0):
+            vmax(b0[:, :, t, :], b0[:, :, t, :], b2[:, :, t, :])
         for b in range(2):
-            nc.vector.tensor_copy(out=zb_bf[:, b, :].rearrange("p (c i t) -> p c t i", i=4, t=PACK),
-                                  in_=b0[:, b].rearrange("p t (c i) -> p c t i", i=4))
+            weave(nc.vector.tensor_copy, zb_bf[:, b * run * PACK : (b + 1) * run * PACK], 0, b0[:, b : b + 1])
         zb_codes = tile("zb_codes", [P, LAST], U32)
         zb_scales = tile("zb_scales", [P, LAST], U8)
         for b in range(2):
-            quantize(zb_codes[:, b * run : (b + 1) * run], zb_scales[:, b * run : (b + 1) * run], zb_bf[:, b, :])
+            quantize(zb_codes[:, b * run : (b + 1) * run], zb_scales[:, b * run : (b + 1) * run], zb_bf[:, b * run * PACK : (b + 1) * run * PACK])
         res = tile("last_out", [P, N // P, LAST], F32)
         for m in range(N // P):
             mx(out_acc[2, m][:], *weights(1, m), zb_codes[:], zb_scales[:], False, True)

@@ -17,17 +17,17 @@ COPY = mybir.ActivationFunctionType.Copy
 MAX = mybir.AluOpType.max
 
 P = 128
+HP = P // 2
 PACK = 4
 K_PASS = P * PACK
 PASSES = K // K_PASS
-RUN = 8
 HALF = T // 2
 FIRST = 384
 LAST = T - FIRST
 ALIGN = 64
-ORDER = (3, 2, 1, 0)
 SPARE = 192
 BLOCK = 64
+GAP = 32
 
 
 def tile_picked_wsagecat_maxrelu_l_kernel(
@@ -57,155 +57,180 @@ def tile_picked_wsagecat_maxrelu_l_kernel(
             )
 
         planes = tile("planes", [P, T], U8)
-        w1_raw = [tile("w1_raw%d" % g, [P, PACK, H], F32) for g in range(PASSES)]
+        w1_raw = {(u, g): tile("w1_raw%d%d" % (u, g), [P, PACK, H // 2], F32)
+                  for u in range(2) for g in range(PASSES)}
         x_codes = [tile("x_codes%d" % g, [P, T], U32) for g in range(PASSES)]
+        offs = [lists.tile([P, T // 16], U16, name="list%d" % d, tag="list%d" % d) for d in range(3)]
 
-        def load_w1(g):
+        def load_w1(u, g):
             nc.sync.dma_start(
-                out=w1_raw[g][:],
-                in_=w1[g * K_PASS : (g + 1) * K_PASS, :].rearrange("(p j) c -> p j c", j=PACK),
+                out=w1_raw[u, g][:],
+                in_=w1[g * K_PASS : (g + 1) * K_PASS, u * (H // 2) : (u + 1) * (H // 2)].rearrange(
+                    "(p j) c -> p j c", j=PACK),
             )
 
-        def load_x(g, c0, c1):
+        def load_x(g):
             nc.sync.dma_start(
-                out=x_codes[g][:, c0:c1].bitcast(I32),
-                in_=x_words[g].rearrange("p n t -> p (n t)")[:, c0 * PACK : c1 * PACK].bitcast(I32),
+                out=x_codes[g][:].bitcast(I32),
+                in_=x_words[g].rearrange("p n t -> p (n t)").bitcast(I32),
             )
 
-        load_w1(0)
+        load_w1(0, 0)
         for q in range(4):
             nc.sync.dma_start(
                 out=planes[32 * q + 4 : 32 * q + 4 + 4 * PASSES, :].bitcast(I32),
                 in_=x_scales[:, 4 * q : 4 * q + 4, :].bitcast(I32),
             )
-        load_x(0, 0, T)
-        load_w1(1)
-        load_x(1, 0, HALF)
-        load_x(1, HALF, T)
-        offs = []
-        for d, pos in enumerate((pos1, pos2, pos3)):
-            lst = lists.tile([P, T // 16], U16, name="list%d" % d, tag="list%d" % d)
-            nc.sync.dma_start(lst[:], pos)
-            offs.append(lst)
-
-        w1_bf = {}
-        w1_codes = {}
-        w1_scales = {}
-        for g in range(PASSES):
-            for t in range(PACK):
-                w1_codes[g, t] = tile("w1_codes%d%d" % (g, t), [P, P], U32)
-                if g == 0:
-                    w1_scales[g, t] = planes[:, t * P : (t + 1) * P]
-                else:
-                    w1_scales[g, t] = tile("w1_scales%d%d" % (g, t), [P, P], U8)[:]
-
-        def round_w1(g, t, engine, tag=None, b0=0, b1=16):
-            if b0 == 0:
-                w1_bf[g, t] = tile("w1_bf%d%d" % (g, t), [P, K_PASS], BF16, tag=tag)
-            src = w1_raw[g][:].rearrange("p j (b t c i) -> p t b c j i", t=PACK, c=2, i=4)[:, t, b0:b1]
-            dst = w1_bf[g, t][:].rearrange("p (b c i j) -> p b c j i", c=2, i=4, j=PACK)[:, b0:b1]
-            if engine == "vector":
-                nc.vector.tensor_copy(out=dst, in_=src)
-            elif engine == "scalar":
-                nc.scalar.copy(out=dst, in_=src)
-            else:
-                nc.scalar.activation(
-                    out=w1_bf[g, t][:].rearrange("p (b r j) -> p b r j", r=RUN, j=PACK),
-                    in_=w1_raw[g][:].rearrange("p j (b t r) -> p t b r j", t=PACK, r=RUN)[:, t],
-                    func=COPY)
-
-        def quantize_w1(g, t):
-            quantize(w1_codes[g, t][:], w1_scales[g, t], w1_bf[g, t][:])
-
-        for t, engine in zip(ORDER, ("vector", "vector", "activation", "scalar")):
-            round_w1(0, t, engine)
-        for t in ORDER:
-            quantize_w1(0, t)
-        round_w1(1, 3, "vector", None, 0, 10)
-        round_w1(1, 3, "scalar", None, 10, 16)
-        quantize_w1(1, 3)
-        round_w1(1, 2, "scalar")
-        round_w1(1, 1, "vector", tag="w1_bf13")
-        quantize_w1(1, 2)
-        quantize_w1(1, 1)
-        round_w1(1, 0, "scalar", tag="w1_bf12")
-        quantize_w1(1, 0)
-
-        w23_raw = tile("w23_raw", [P, 2, PACK, N], F32, tag="w1_raw0")
+        load_w1(0, 1)
+        load_x(0)
+        load_x(1)
+        nc.sync.dma_start(offs[0][:], pos1)
+        nc.sync.dma_start(offs[1][:], pos2)
+        nc.sync.dma_start(offs[2][:], pos3)
+        load_w1(1, 0)
+        load_w1(1, 1)
+        w23_raw = tile("w23_raw", [P, 2, PACK, N], F32)
         for s, w in enumerate((w2, w3)):
             for t in range(PACK):
                 nc.sync.dma_start(
                     out=w23_raw[:, s, t, :],
-                    in_=w.rearrange("(b t r) n -> t b r n", t=PACK, r=RUN)[t],
+                    in_=w.rearrange("(a t i) n -> t a i n", t=PACK, i=4)[t],
                 )
 
-        h = tile("h", [P, PACK * T + SPARE], F32)
-        nc.gpsimd.memset(h[:, PACK * T :], 0.0)
-        h_groups = [(ORDER[0], 0, HALF), (ORDER[0], HALF, T)] + [(t, 0, T) for t in ORDER[1:]]
-        h_acc = [ps.tile([P, c1 - c0], F32, name="h_acc%d" % i, tag="bank%d" % i)
-                 for i, (t, c0, c1) in enumerate(h_groups)]
+        def raw_view(u, g):
+            return w1_raw[u, g][:].rearrange("p j (a t i) -> p t a j i", t=PACK, i=4)
+
+        def pair_view(values):
+            return values.rearrange("p (t a i j) -> p t a j i", t=2, i=4, j=PACK)
+
+        lo_bf = [tile("lo_bf%d" % g, [P, K_PASS], BF16) for g in range(PASSES)]
+        lo_codes = tile("lo_codes", [P, PASSES * P], U32)
+        hi_bf = tile("hi_bf", [P, PASSES * K_PASS], BF16)
+        hi_codes = tile("hi_codes", [P, PASSES * P], U32)
+        hi_scales = tile("hi_scales", [P, PASSES * P], U8)
+        nat_bf = tile("nat_bf", [P, PASSES * 2 * K_PASS], BF16)
+        nat_codes = tile("nat_codes", [P, PASSES * 2 * P], U32)
+        nat_scales = tile("nat_scales", [P, PASSES * 2 * P], U8)
+        nat_view = nat_bf[:].rearrange("p (g t u a i j) -> p g u t a j i", g=PASSES, t=2, u=2, i=4, j=PACK)
+
         for g in range(PASSES):
-            for acc, (t, c0, c1) in zip(h_acc, h_groups):
-                mx(acc[:], w1_codes[g, t][:], w1_scales[g, t],
-                   x_codes[g][:, c0:c1], planes[4 + 4 * g : P, c0:c1], g == 0, g == PASSES - 1)
-                if g == PASSES - 1 and c0 == HALF:
-                    nc.vector.tensor_scalar(out=h[:, t * T + c0 : t * T + c1], in0=acc[:], scalar1=0.0, scalar2=None, op0=MAX)
-                elif g == PASSES - 1:
-                    nc.scalar.activation(out=h[:, t * T + c0 : t * T + c1], in_=acc[:], func=RELU)
+            nc.vector.tensor_copy(out=pair_view(lo_bf[g][:]), in_=raw_view(0, g)[:, 0:2])
+            if g == 0:
+                for t in range(2):
+                    nc.scalar.activation(out=nat_view[:, g, 0, t], in_=raw_view(0, g)[:, 2 + t], func=COPY)
+            else:
+                nc.scalar.copy(out=nat_view[:, g, 0], in_=raw_view(0, g)[:, 2:4])
+            quantize(lo_codes[:, g * P : (g + 1) * P], planes[:, g * P : (g + 1) * P], lo_bf[g][:])
 
-        h_bf = tile("h_bf", [P, T * PACK], BF16)
-        nc.scalar.copy(out=h_bf[:].rearrange("p (c i t) -> p c t i", i=4, t=PACK),
-                       in_=h[:, 0 : PACK * T].rearrange("p (t c i) -> p c t i", t=PACK, i=4))
-        w23_bf = tile("w23_bf", [P, 2, N * PACK], BF16)
-        for s in range(2):
-            nc.scalar.copy(out=w23_bf[:, s, :].rearrange("p (c i t) -> p c t i", i=4, t=PACK),
-                           in_=w23_raw[:, s].rearrange("p t (c i) -> p c t i", i=4))
+        h = tile("h", [P, (PACK + 2) * T + SPARE], F32)
+        nc.gpsimd.memset(h[:, (PACK + 2) * T :], 0.0)
+        place = (5, 4, 2, 3)
 
-        def gather(dst, t, d, v0, v1):
+        def h_cols(w, c0=0, c1=T):
+            return slice(place[w] * T + c0, place[w] * T + c1)
+
+        def project(w, codes, scales, col, groups, bank):
+            accs = [ps.tile([P, c1 - c0], F32, name="h_acc%d%d" % (w, i), tag="bank%d" % (bank + i))
+                    for i, (c0, c1) in enumerate(groups)]
+            for g in range(PASSES):
+                for acc, (c0, c1) in zip(accs, groups):
+                    mx(acc[:], codes[:, col(g) : col(g) + P], scales[:, col(g) : col(g) + P],
+                       x_codes[g][:, c0:c1], planes[4 + 4 * g : P, c0:c1], g == 0, g == PASSES - 1)
+                    if g == PASSES - 1 and w == 0 and c0 == HALF:
+                        nc.vector.tensor_scalar(out=h[:, h_cols(w, c0, c1)], in0=acc[:], scalar1=0.0,
+                                                scalar2=None, op0=MAX)
+                    elif g == PASSES - 1:
+                        nc.scalar.activation(out=h[:, h_cols(w, c0, c1)], in_=acc[:], func=RELU)
+
+        halves = [(0, HALF), (HALF, T)]
+        project(0, lo_codes, planes, lambda g: g * P, halves, 0)
+
+        def gather(dst, w, d, v0, v1):
             width = T + SPARE if v1 - v0 == T else T
-            window = h[:, t * T : t * T + width]
-            nc.vector.tensor_copy(out=dst, in_=window.indirect(offs[d][:, v0 // 16 : v1 // 16]))
+            start = h_cols(w).start
+            nc.vector.tensor_copy(out=dst, in_=h[:, start : start + width].indirect(offs[d][:, v0 // 16 : v1 // 16]))
 
         def vmax(dst, one, other):
             nc.vector.tensor_tensor(out=dst, in0=one, in1=other, op=MAX)
 
-        nb = T // BLOCK
+        def gapped(name, tag=None):
+            return tile(name, [P, 2, HALF + GAP], BF16, tag=tag)[:, :, 0:HALF]
+
+        e = [tile("e%d" % d, [P, 2, 2, HALF + GAP], BF16)[:, :, :, 0:HALF] for d in range(2)]
+        gather(e[0][:, 0], 0, 0, 0, T)
+        gather(e[1][:, 0], 0, 1, 0, T)
+        for g in range(PASSES):
+            nc.scalar.copy(out=pair_view(hi_bf[:, g * K_PASS : (g + 1) * K_PASS]), in_=raw_view(1, g)[:, 0:2])
+        quantize(hi_codes[:], hi_scales[:], hi_bf[:])
+        for g in range(PASSES):
+            nc.scalar.copy(out=nat_view[:, g, 1], in_=raw_view(1, g)[:, 2:4])
+        late = tile("late", [P, 2, 2, 2, HALF + GAP], BF16, tag="w1_raw11")[:, :, :, :, 0:HALF]
+        two = late[:, 0]
+        third = late[:, 1]
+        vmax(two[:, 0], e[0][:, 0], e[1][:, 0])
+        gather(third[:, 0], 0, 2, 0, T)
+        project(1, hi_codes, hi_scales, lambda g: g * P, halves, 2)
+        quantize(nat_codes[:], nat_scales[:], nat_bf[:])
+        gather(e[0][:, 1], 1, 0, 0, T)
+        gather(e[1][:, 1], 1, 1, 0, T)
+        gather(third[:, 1], 1, 2, 0, T)
+        vmax(two[:, 1], e[0][:, 1], e[1][:, 1])
+        for w in (2, 3):
+            project(w, nat_codes, nat_scales, lambda g: (2 * g + w - 2) * P, [(0, T)], 2 + w)
         na = FIRST // BLOCK
+        a0 = tile("a0", [P, na, 2, BLOCK], BF16)
+        gather(a0[:, :, 0, :], 2, 0, 0, FIRST)
+        zm = tile("zm", [P, 2, T], BF16)
+        vmax(zm[:].rearrange("p w (a v) -> p w a v", a=2), two, third)
+
+        z01 = tile("z01", [P, 2, T], BF16)
+        for w in range(2):
+            for t in range(2):
+                nc.sync.dma_start(out=h[w * HP : (w + 1) * HP, t * T : (t + 1) * T], in_=h[t * HP : (t + 1) * HP, h_cols(w)])
+        for w in range(2):
+            for t in range(2):
+                nc.sync.dma_start(out=z01[w * HP : (w + 1) * HP, t, :], in_=zm[t * HP : (t + 1) * HP, w, :])
+
+        def weave(copy, dst, t0, pair):
+            copy(out=dst.rearrange("p (c i t) -> p c t i", i=4, t=PACK)[:, :, t0 : t0 + 2, :],
+                 in_=pair.rearrange("p t (c i) -> p c t i", i=4))
+
+        w23_bf = tile("w23_bf", [P, 2, N * PACK], BF16)
+        for s in range(2):
+            nc.scalar.copy(out=w23_bf[:, s, :].rearrange("p (c i t) -> p c t i", i=4, t=PACK),
+                           in_=w23_raw[:, s].rearrange("p t (c i) -> p c t i", i=4))
+        h_bf = tile("h_bf", [P, T * PACK], BF16)
+        nc.scalar.copy(out=h_bf[:].rearrange("p (c i t) -> p c t i", i=4, t=PACK),
+                       in_=h[:, 0 : PACK * T].rearrange("p (t c i) -> p c t i", t=PACK, i=4))
+        za_bf = tile("za_bf", [P, FIRST * PACK], BF16)
+        zb_bf = tile("zb_bf", [P, LAST * PACK], BF16)
+        weave(nc.scalar.copy, za_bf[:], 0, z01[:, :, 0:FIRST])
+        weave(nc.scalar.copy, zb_bf[:], 0, z01[:, :, FIRST:T])
+
         h_codes = tile("h_codes", [P, T], U32)
         h_scales = tile("h_scales", [P, T], U8)
         w23_codes = tile("w23_codes", [P, 2 * N], U32)
         w23_scales = tile("w23_scales", [P, 2 * N], U8)
-        za_bf = tile("za_bf", [P, FIRST * PACK], BF16)
-        zb_bf = tile("zb_bf", [P, LAST * PACK], BF16)
 
-        def weave(copy, dst, t0, pair):
-            copy(out=dst.rearrange("p (b c i t) -> p b c t i", c=BLOCK // 4, i=4, t=PACK)[:, :, :, t0 : t0 + 2, :],
+        def weave_blocks(copy, dst, pair):
+            copy(out=dst.rearrange("p (b c i t) -> p b c t i", c=BLOCK // 4, i=4, t=PACK)[:, :, :, 2:4, :],
                  in_=pair.rearrange("p b t (c i) -> p b c t i", i=4))
 
-        e = [tile("e%d" % d, [P, nb, 2, BLOCK], BF16) for d in range(3)]
-        a0 = tile("a0", [P, na, 2, BLOCK], BF16)
-        for t in (3, 2):
-            for d in range(3):
-                gather(e[d][:, :, t - 2, :], t, d, 0, T)
-        vmax(e[0][:], e[0][:], e[1][:])
-        gather(a0[:, :, 1, :], 1, 0, 0, FIRST)
-        vmax(e[0][:], e[0][:], e[2][:])
-        weave(nc.scalar.copy, za_bf[:], 2, e[0][:, 0:na])
-        weave(nc.scalar.copy, zb_bf[:], 2, e[0][:, na:nb])
-
-        gather(a0[:, :, 0, :], 0, 0, 0, FIRST)
-        quantize(h_codes[:], h_scales[:], h_bf[:])
-        a2 = tile("a2", [P, na, 2, BLOCK], BF16)
-        for t in (1, 0):
-            gather(a2[:, :, t, :], t, 2, 0, FIRST)
+        a1 = tile("a1", [P, na, 2, BLOCK], BF16)
+        gather(a0[:, :, 1, :], 3, 0, 0, FIRST)
+        for t in range(2):
+            gather(a1[:, :, t, :], 2 + t, 1, 0, FIRST)
         quantize(w23_codes[:], w23_scales[:], w23_bf[:].rearrange("p s c -> p (s c)"))
-        vmax(a0[:], a0[:], a2[:])
-        a1 = tile("a1", [P, na, 2, BLOCK], BF16, tag="w23_bf")
-        for t in (1, 0):
-            gather(a1[:, :, t, :], t, 1, 0, FIRST)
-        for t in (1, 0):
-            vmax(a0[:, :, t, :], a0[:, :, t, :], a1[:, :, t, :])
-        weave(nc.scalar.copy, za_bf[:], 0, a0[:])
+        am = tile("am", [P, na, 2, BLOCK], BF16, tag="w23_raw")
+        vmax(am[:], a0[:], a1[:])
+        quantize(h_codes[:], h_scales[:], h_bf[:])
+        a2 = h[:, 0:FIRST].bitcast(BF16).rearrange("p (b t v) -> p b t v", t=2, v=BLOCK)
+        for t in range(2):
+            gather(a2[:, :, t, :], 2 + t, 2, 0, FIRST)
+        for t in range(2):
+            vmax(am[:, :, t, :], am[:, :, t, :], a2[:, :, t, :])
+        weave_blocks(nc.scalar.copy, za_bf[:, 0 : HALF * PACK], am[:, 0:4])
+        weave_blocks(nc.scalar.copy, za_bf[:, HALF * PACK :], am[:, 4:na])
 
         def weights(s, m):
             cols = slice(s * N + m * P, s * N + (m + 1) * P)
@@ -219,18 +244,20 @@ def tile_picked_wsagecat_maxrelu_l_kernel(
                 mx(acc[:], *weights(0, m), h_codes[:, c0:c1], h_scales[:, c0:c1], True, False)
                 out_acc[i, m] = acc
 
-        run = BLOCK
-        b01 = tile("b01", [P, 2, 2, 2, BLOCK], BF16, tag="w23_bf")
-        b0 = b01[:, 0]
+        b01 = h[:, T + BLOCK : T + BLOCK + HALF].bitcast(BF16).rearrange("p (d b t v) -> p d b t v", d=2, b=2, t=2)
         for d in range(2):
-            for t in (1, 0):
-                gather(b01[:, d, :, t, :], t, d, FIRST, T)
-        vmax(b0, b0, b01[:, 1])
+            for t in range(2):
+                gather(b01[:, d, :, t, :], 2 + t, d, FIRST, T)
 
         za_codes = tile("za_codes", [P, FIRST], U32)
         za_scales = tile("za_scales", [P, FIRST], U8)
+        tail = tile("tail", [P, 2, 2, 2, BLOCK], BF16, tag="w23_raw")
+        b0 = tail[:, 0]
+        b2 = tail[:, 1]
         for c0, c1 in groups[:2]:
             quantize(za_codes[:, c0:c1], za_scales[:, c0:c1], za_bf[:, c0 * PACK : c1 * PACK])
+            if c0 == 0:
+                vmax(b0, b01[:, 0], b01[:, 1])
 
         for m in range(N // P):
             res = tile("first_out%d" % m, [P, FIRST], F32)
@@ -240,17 +267,17 @@ def tile_picked_wsagecat_maxrelu_l_kernel(
                 nc.scalar.activation(out=res[:, c0:c1], in_=acc[:], func=RELU)
             nc.sync.dma_start(out=out[m * P : (m + 1) * P, 0:FIRST], in_=res[:])
 
-        b2 = tile("b2", [P, 2, 2, BLOCK], BF16, tag="za_bf")
-        for t in (1, 0):
-            gather(b2[:, :, t, :], t, 2, FIRST, T)
-        for t in (1, 0):
+        for t in range(2):
+            gather(b2[:, :, t, :], 2 + t, 2, FIRST, T)
+        for t in range(2):
             vmax(b0[:, :, t, :], b0[:, :, t, :], b2[:, :, t, :])
         for b in range(2):
-            weave(nc.vector.tensor_copy, zb_bf[:, b * run * PACK : (b + 1) * run * PACK], 0, b0[:, b : b + 1])
+            weave_blocks(nc.vector.tensor_copy, zb_bf[:, b * BLOCK * PACK : (b + 1) * BLOCK * PACK], b0[:, b : b + 1])
         zb_codes = tile("zb_codes", [P, LAST], U32)
         zb_scales = tile("zb_scales", [P, LAST], U8)
         for b in range(2):
-            quantize(zb_codes[:, b * run : (b + 1) * run], zb_scales[:, b * run : (b + 1) * run], zb_bf[:, b * run * PACK : (b + 1) * run * PACK])
+            quantize(zb_codes[:, b * BLOCK : (b + 1) * BLOCK], zb_scales[:, b * BLOCK : (b + 1) * BLOCK],
+                     zb_bf[:, b * BLOCK * PACK : (b + 1) * BLOCK * PACK])
         res = tile("last_out", [P, N // P, LAST], F32)
         for m in range(N // P):
             mx(out_acc[2, m][:], *weights(1, m), zb_codes[:], zb_scales[:], False, True)

@@ -37,6 +37,7 @@ def tile_picked_wsagecat_maxrelu_l_kernel(
     with ExitStack() as ctx:
         lists = ctx.enter_context(tc.tile_pool(name="lists", bufs=1))
         sb = ctx.enter_context(tc.tile_pool(name="sb", bufs=1))
+        reuse = ctx.enter_context(tc.tile_pool(name="reuse", bufs=1))
         ps = ctx.enter_context(tc.psum_pool(name="ps", bufs=1))
 
         def tile(name, shape, dtype, tag=None):
@@ -56,54 +57,64 @@ def tile_picked_wsagecat_maxrelu_l_kernel(
                 stop=stop,
             )
 
-        planes = tile("planes", [P, T], U8)
-        w1_raw = {(u, g): tile("w1_raw%d%d" % (u, g), [P, PACK, H // 2], F32)
-                  for u in range(2) for g in range(PASSES)}
+        x_planes = tile("x_planes", [P, PASSES, T], U8)
+        raw_cols = PACK * H // 2
+        w1_raw = {(0, g): tile("w1_raw0%d" % g, [P, raw_cols], F32)[:] for g in range(PASSES)}
+        hi_raw = tile("hi_raw", [P, PASSES * raw_cols], F32)
+        for g in range(PASSES):
+            w1_raw[1, g] = hi_raw[:, (1 - g) * raw_cols : (2 - g) * raw_cols]
         x_codes = [tile("x_codes%d" % g, [P, T], U32) for g in range(PASSES)]
         offs = [lists.tile([P, T // 16], U16, name="list%d" % d, tag="list%d" % d) for d in range(3)]
 
         def load_w1(u, g):
             nc.sync.dma_start(
-                out=w1_raw[u, g][:],
+                out=w1_raw[u, g].rearrange("p (j c) -> p j c", j=PACK),
                 in_=w1[g * K_PASS : (g + 1) * K_PASS, u * (H // 2) : (u + 1) * (H // 2)].rearrange(
                     "(p j) c -> p j c", j=PACK),
             )
 
-        def load_x(g):
+        def load_x(g, c0, c1):
             nc.sync.dma_start(
-                out=x_codes[g][:].bitcast(I32),
-                in_=x_words[g].rearrange("p n t -> p (n t)").bitcast(I32),
+                out=x_codes[g][:, c0:c1].bitcast(I32),
+                in_=x_words[g].rearrange("p n t -> p (n t)")[:, c0 * PACK : c1 * PACK].bitcast(I32),
             )
 
-        load_w1(0, 0)
-        for q in range(4):
+        def load_scales(q):
             nc.sync.dma_start(
-                out=planes[32 * q + 4 : 32 * q + 4 + 4 * PASSES, :].bitcast(I32),
-                in_=x_scales[:, 4 * q : 4 * q + 4, :].bitcast(I32),
+                out=x_planes[32 * q : 32 * q + 4].bitcast(I32),
+                in_=x_scales[:, 4 * q : 4 * q + 4, :].rearrange("g j c -> j g c").bitcast(I32),
             )
+
+        load_scales(0)
+        load_scales(1)
+        load_w1(0, 0)
+        load_scales(2)
+        load_scales(3)
         load_w1(0, 1)
-        load_x(0)
-        load_x(1)
+        for g in range(PASSES):
+            load_x(g, 0, HALF)
+            load_x(g, HALF, T)
         nc.sync.dma_start(offs[0][:], pos1)
-        nc.sync.dma_start(offs[1][:], pos2)
-        nc.sync.dma_start(offs[2][:], pos3)
         load_w1(1, 0)
+        nc.sync.dma_start(offs[1][:], pos2)
         load_w1(1, 1)
+        nc.sync.dma_start(offs[2][:], pos3)
         w23_raw = tile("w23_raw", [P, 2, PACK, N], F32)
         for s, w in enumerate((w2, w3)):
-            for t in range(PACK):
+            for u in range(2):
                 nc.sync.dma_start(
-                    out=w23_raw[:, s, t, :],
-                    in_=w.rearrange("(a t i) n -> t a i n", t=PACK, i=4)[t],
+                    out=w23_raw[:, s, 2 * u : 2 * u + 2, :].rearrange("p e n -> p (e n)"),
+                    in_=w.rearrange("(a u i e) n -> u a i (e n)", u=2, i=4, e=2)[u],
                 )
 
         def raw_view(u, g):
-            return w1_raw[u, g][:].rearrange("p j (a t i) -> p t a j i", t=PACK, i=4)
+            return w1_raw[u, g].rearrange("p (j a v i e) -> p v e a j i", j=PACK, v=2, i=4, e=2)
 
         def pair_view(values):
             return values.rearrange("p (t a i j) -> p t a j i", t=2, i=4, j=PACK)
 
         lo_bf = [tile("lo_bf%d" % g, [P, K_PASS], BF16) for g in range(PASSES)]
+        lo_scales = tile("lo_scales", [P, PASSES * P], U8)
         lo_codes = tile("lo_codes", [P, PASSES * P], U32)
         hi_bf = tile("hi_bf", [P, PASSES * K_PASS], BF16)
         hi_codes = tile("hi_codes", [P, PASSES * P], U32)
@@ -114,13 +125,13 @@ def tile_picked_wsagecat_maxrelu_l_kernel(
         nat_view = nat_bf[:].rearrange("p (g t u a i j) -> p g u t a j i", g=PASSES, t=2, u=2, i=4, j=PACK)
 
         for g in range(PASSES):
-            nc.vector.tensor_copy(out=pair_view(lo_bf[g][:]), in_=raw_view(0, g)[:, 0:2])
+            nc.vector.tensor_copy(out=pair_view(lo_bf[g][:]), in_=raw_view(0, g)[:, 0])
             if g == 0:
                 for t in range(2):
-                    nc.scalar.activation(out=nat_view[:, g, 0, t], in_=raw_view(0, g)[:, 2 + t], func=COPY)
+                    nc.scalar.activation(out=nat_view[:, g, 0, t], in_=raw_view(0, g)[:, 1, t], func=COPY)
             else:
-                nc.scalar.copy(out=nat_view[:, g, 0], in_=raw_view(0, g)[:, 2:4])
-            quantize(lo_codes[:, g * P : (g + 1) * P], planes[:, g * P : (g + 1) * P], lo_bf[g][:])
+                nc.scalar.copy(out=nat_view[:, g, 0], in_=raw_view(0, g)[:, 1])
+            quantize(lo_codes[:, g * P : (g + 1) * P], lo_scales[:, g * P : (g + 1) * P], lo_bf[g][:])
 
         h = tile("h", [P, (PACK + 2) * T + SPARE], F32)
         nc.gpsimd.memset(h[:, (PACK + 2) * T :], 0.0)
@@ -135,7 +146,7 @@ def tile_picked_wsagecat_maxrelu_l_kernel(
             for g in range(PASSES):
                 for acc, (c0, c1) in zip(accs, groups):
                     mx(acc[:], codes[:, col(g) : col(g) + P], scales[:, col(g) : col(g) + P],
-                       x_codes[g][:, c0:c1], planes[4 + 4 * g : P, c0:c1], g == 0, g == PASSES - 1)
+                       x_codes[g][:, c0:c1], x_planes[:, g, c0:c1], g == 0, g == PASSES - 1)
                     if g == PASSES - 1 and w == 0 and c0 == HALF:
                         nc.vector.tensor_scalar(out=h[:, h_cols(w, c0, c1)], in0=acc[:], scalar1=0.0,
                                                 scalar2=None, op0=MAX)
@@ -143,7 +154,7 @@ def tile_picked_wsagecat_maxrelu_l_kernel(
                         nc.scalar.activation(out=h[:, h_cols(w, c0, c1)], in_=acc[:], func=RELU)
 
         halves = [(0, HALF), (HALF, T)]
-        project(0, lo_codes, planes, lambda g: g * P, halves, 0)
+        project(0, lo_codes, lo_scales, lambda g: g * P, halves, 0)
 
         def gather(dst, w, d, v0, v1):
             width = T + SPARE if v1 - v0 == T else T
@@ -153,18 +164,15 @@ def tile_picked_wsagecat_maxrelu_l_kernel(
         def vmax(dst, one, other):
             nc.vector.tensor_tensor(out=dst, in0=one, in1=other, op=MAX)
 
-        def gapped(name, tag=None):
-            return tile(name, [P, 2, HALF + GAP], BF16, tag=tag)[:, :, 0:HALF]
-
-        e = [tile("e%d" % d, [P, 2, 2, HALF + GAP], BF16)[:, :, :, 0:HALF] for d in range(2)]
+        e = [tile("e%d" % d, [P, 2, 32, 32], BF16)[:, :, :, 0:16] for d in range(2)]
         gather(e[0][:, 0], 0, 0, 0, T)
         gather(e[1][:, 0], 0, 1, 0, T)
         for g in range(PASSES):
-            nc.scalar.copy(out=pair_view(hi_bf[:, g * K_PASS : (g + 1) * K_PASS]), in_=raw_view(1, g)[:, 0:2])
+            nc.scalar.copy(out=pair_view(hi_bf[:, g * K_PASS : (g + 1) * K_PASS]), in_=raw_view(1, g)[:, 0])
         quantize(hi_codes[:], hi_scales[:], hi_bf[:])
         for g in range(PASSES):
-            nc.scalar.copy(out=nat_view[:, g, 1], in_=raw_view(1, g)[:, 2:4])
-        late = tile("late", [P, 2, 2, 2, HALF + GAP], BF16, tag="w1_raw11")[:, :, :, :, 0:HALF]
+            nc.scalar.copy(out=nat_view[:, g, 1], in_=raw_view(1, g)[:, 1])
+        late = hi_raw[:].bitcast(BF16).rearrange("p (w k r v) -> p k w r v", w=2, k=2, v=32)[:, :, :, :, 0:16]
         two = late[:, 0]
         third = late[:, 1]
         vmax(two[:, 0], e[0][:, 0], e[1][:, 0])
@@ -175,15 +183,16 @@ def tile_picked_wsagecat_maxrelu_l_kernel(
         gather(e[1][:, 1], 1, 1, 0, T)
         gather(third[:, 1], 1, 2, 0, T)
         vmax(two[:, 1], e[0][:, 1], e[1][:, 1])
-        for w in (2, 3):
-            project(w, nat_codes, nat_scales, lambda g: (2 * g + w - 2) * P, [(0, T)], 2 + w)
+        for w, groups in ((3, halves), (2, [(0, T)])):
+            project(w, nat_codes, nat_scales, lambda g: (2 * g + w - 2) * P, groups, 4)
+        nb = T // BLOCK
         na = FIRST // BLOCK
-        a0 = tile("a0", [P, na, 2, BLOCK], BF16)
-        gather(a0[:, :, 0, :], 2, 0, 0, FIRST)
-        zm = tile("zm", [P, 2, T], BF16)
-        vmax(zm[:].rearrange("p w (a v) -> p w a v", a=2), two, third)
+        f = [tile("f%d" % d, [P, nb, 2, BLOCK], BF16) for d in range(2)]
+        gather(f[0][:, :, 1, :], 3, 0, 0, T)
+        zm = tile("zm", [P, 2, T], BF16, tag="x_codes0")
+        vmax(zm[:].rearrange("p w (r v) -> p w r v", v=16), two, third)
 
-        z01 = tile("z01", [P, 2, T], BF16)
+        z01 = reuse.tile([P, 2, 2 * FIRST], BF16, name="z01", offset=0, align_bytes=ALIGN)[:, :, 0:T]
         for w in range(2):
             for t in range(2):
                 nc.sync.dma_start(out=h[w * HP : (w + 1) * HP, t * T : (t + 1) * T], in_=h[t * HP : (t + 1) * HP, h_cols(w)])
@@ -191,96 +200,73 @@ def tile_picked_wsagecat_maxrelu_l_kernel(
             for t in range(2):
                 nc.sync.dma_start(out=z01[w * HP : (w + 1) * HP, t, :], in_=zm[t * HP : (t + 1) * HP, w, :])
 
-        def weave(copy, dst, t0, pair):
-            copy(out=dst.rearrange("p (c i t) -> p c t i", i=4, t=PACK)[:, :, t0 : t0 + 2, :],
-                 in_=pair.rearrange("p t (c i) -> p c t i", i=4))
-
-        w23_bf = tile("w23_bf", [P, 2, N * PACK], BF16)
+        wh_bf = tile("wh_bf", [P, (2 * N + T) * PACK], BF16)
         for s in range(2):
-            nc.scalar.copy(out=w23_bf[:, s, :].rearrange("p (c i t) -> p c t i", i=4, t=PACK),
+            nc.scalar.copy(out=wh_bf[:, s * N * PACK : (s + 1) * N * PACK].rearrange("p (c i t) -> p c t i", i=4, t=PACK),
                            in_=w23_raw[:, s].rearrange("p t (c i) -> p c t i", i=4))
-        h_bf = tile("h_bf", [P, T * PACK], BF16)
-        nc.scalar.copy(out=h_bf[:].rearrange("p (c i t) -> p c t i", i=4, t=PACK),
+        nc.scalar.copy(out=wh_bf[:, 2 * N * PACK :].rearrange("p (c i t) -> p c t i", i=4, t=PACK),
                        in_=h[:, 0 : PACK * T].rearrange("p (t c i) -> p c t i", t=PACK, i=4))
-        za_bf = tile("za_bf", [P, FIRST * PACK], BF16)
-        zb_bf = tile("zb_bf", [P, LAST * PACK], BF16)
-        weave(nc.scalar.copy, za_bf[:], 0, z01[:, :, 0:FIRST])
-        weave(nc.scalar.copy, zb_bf[:], 0, z01[:, :, FIRST:T])
+        z_bf = h[:, 0 : 2 * T].bitcast(BF16)
+        nc.scalar.copy(out=z_bf.rearrange("p (c i t) -> p c t i", i=4, t=PACK)[:, :, 0:2, :],
+                       in_=z01.rearrange("p t (c i) -> p c t i", i=4))
 
-        h_codes = tile("h_codes", [P, T], U32)
-        h_scales = tile("h_scales", [P, T], U8)
-        w23_codes = tile("w23_codes", [P, 2 * N], U32)
-        w23_scales = tile("w23_scales", [P, 2 * N], U8)
+        def weave_blocks(dst, pair):
+            nc.scalar.copy(
+                out=dst.rearrange("p (b c i t) -> p b c t i", c=BLOCK // 4, i=4, t=PACK)[:, :, :, 2:4, :],
+                in_=pair.rearrange("p b t (c i) -> p b c t i", i=4))
 
-        def weave_blocks(copy, dst, pair):
-            copy(out=dst.rearrange("p (b c i t) -> p b c t i", c=BLOCK // 4, i=4, t=PACK)[:, :, :, 2:4, :],
-                 in_=pair.rearrange("p b t (c i) -> p b c t i", i=4))
-
-        a1 = tile("a1", [P, na, 2, BLOCK], BF16)
-        gather(a0[:, :, 1, :], 3, 0, 0, FIRST)
-        for t in range(2):
-            gather(a1[:, :, t, :], 2 + t, 1, 0, FIRST)
-        quantize(w23_codes[:], w23_scales[:], w23_bf[:].rearrange("p s c -> p (s c)"))
-        am = tile("am", [P, na, 2, BLOCK], BF16, tag="w23_raw")
-        vmax(am[:], a0[:], a1[:])
-        quantize(h_codes[:], h_scales[:], h_bf[:])
-        a2 = h[:, 0:FIRST].bitcast(BF16).rearrange("p (b t v) -> p b t v", t=2, v=BLOCK)
-        for t in range(2):
+        a2 = tile("a2", [P, na, 2, BLOCK], BF16)
+        zn = f[0]
+        for t in (1, 0):
+            if t == 0:
+                gather(f[0][:, :, t, :], 2 + t, 0, 0, T)
+            gather(f[1][:, :, t, :], 2 + t, 1, 0, T)
             gather(a2[:, :, t, :], 2 + t, 2, 0, FIRST)
-        for t in range(2):
-            vmax(am[:, :, t, :], am[:, :, t, :], a2[:, :, t, :])
-        weave_blocks(nc.scalar.copy, za_bf[:, 0 : HALF * PACK], am[:, 0:4])
-        weave_blocks(nc.scalar.copy, za_bf[:, HALF * PACK :], am[:, 4:na])
+            vmax(zn[:, :, t, :], zn[:, :, t, :], f[1][:, :, t, :])
+        za = reuse.tile([P, nb, 2, BLOCK], BF16, name="za", offset=0, align_bytes=ALIGN)
+        for t in (1, 0):
+            vmax(za[:, 0:na, t, :], zn[:, 0:na, t, :], a2[:, :, t, :])
+        weave_blocks(z_bf[:, 0 : HALF * PACK], za[:, 0:4])
+        weave_blocks(z_bf[:, HALF * PACK : FIRST * PACK], za[:, 4:na])
+        wh_codes = tile("wh_codes", [P, 2 * N + T], U32)
+        wh_scales = reuse.tile([P, 2 * N + T], U8, name="wh_scales", offset=4 * T, align_bytes=ALIGN)
+        quantize(wh_codes[:], wh_scales[:], wh_bf[:])
 
         def weights(s, m):
             cols = slice(s * N + m * P, s * N + (m + 1) * P)
-            return w23_codes[:, cols], w23_scales[:, cols]
+            return wh_codes[:, cols], wh_scales[:, cols]
 
         groups = [(0, HALF), (HALF, FIRST), (FIRST, T)]
+        banks = (0, 1, 2, 3, 6, 7)
         out_acc = {}
         for i, (c0, c1) in enumerate(groups):
             for m in range(N // P):
-                acc = ps.tile([P, c1 - c0], F32, name="out_acc%d%d" % (i, m), tag="bank%d" % (2 * i + m))
-                mx(acc[:], *weights(0, m), h_codes[:, c0:c1], h_scales[:, c0:c1], True, False)
+                acc = ps.tile([P, c1 - c0], F32, name="out_acc%d%d" % (i, m), tag="bank%d" % banks[2 * i + m])
+                mx(acc[:], *weights(0, m), wh_codes[:, 2 * N + c0 : 2 * N + c1], wh_scales[:, 2 * N + c0 : 2 * N + c1], True, False)
                 out_acc[i, m] = acc
 
-        b01 = h[:, T + BLOCK : T + BLOCK + HALF].bitcast(BF16).rearrange("p (d b t v) -> p d b t v", d=2, b=2, t=2)
-        for d in range(2):
-            for t in range(2):
-                gather(b01[:, d, :, t, :], 2 + t, d, FIRST, T)
-
-        za_codes = tile("za_codes", [P, FIRST], U32)
-        za_scales = tile("za_scales", [P, FIRST], U8)
-        tail = tile("tail", [P, 2, 2, 2, BLOCK], BF16, tag="w23_raw")
-        b0 = tail[:, 0]
-        b2 = tail[:, 1]
-        for c0, c1 in groups[:2]:
-            quantize(za_codes[:, c0:c1], za_scales[:, c0:c1], za_bf[:, c0 * PACK : c1 * PACK])
-            if c0 == 0:
-                vmax(b0, b01[:, 0], b01[:, 1])
-
-        for m in range(N // P):
-            res = tile("first_out%d" % m, [P, FIRST], F32)
-            for i, (c0, c1) in enumerate(groups[:2]):
+        z_codes = tile("z_codes", [P, T], U32)
+        z_scales = tile("z_scales", [P, T], U8)
+        b2 = za[:].rearrange("p (t b) s v -> p t b s v", t=2)[:, :, 0:2, 0, :]
+        for i, (c0, c1) in enumerate(groups[:2]):
+            if i == 1:
+                gather(b2[:, i], 2 + i, 2, FIRST, T)
+            quantize(z_codes[:, c0:c1], z_scales[:, c0:c1], z_bf[:, c0 * PACK : c1 * PACK])
+            if i == 0:
+                gather(b2[:, i], 2 + i, 2, FIRST, T)
+            for m in range(N // P):
+                res = tile("first_out%d%d" % (i, m), [P, c1 - c0], F32)
                 acc = out_acc[i, m]
-                mx(acc[:], *weights(1, m), za_codes[:, c0:c1], za_scales[:, c0:c1], False, True)
-                nc.scalar.activation(out=res[:, c0:c1], in_=acc[:], func=RELU)
-            nc.sync.dma_start(out=out[m * P : (m + 1) * P, 0:FIRST], in_=res[:])
+                mx(acc[:], *weights(1, m), z_codes[:, c0:c1], z_scales[:, c0:c1], False, True)
+                nc.scalar.activation(out=res[:], in_=acc[:], func=RELU)
+                nc.sync.dma_start(out=out[m * P : (m + 1) * P, c0:c1], in_=res[:])
 
-        for t in range(2):
-            gather(b2[:, :, t, :], 2 + t, 2, FIRST, T)
-        for t in range(2):
-            vmax(b0[:, :, t, :], b0[:, :, t, :], b2[:, :, t, :])
-        for b in range(2):
-            weave_blocks(nc.vector.tensor_copy, zb_bf[:, b * BLOCK * PACK : (b + 1) * BLOCK * PACK], b0[:, b : b + 1])
-        zb_codes = tile("zb_codes", [P, LAST], U32)
-        zb_scales = tile("zb_scales", [P, LAST], U8)
-        for b in range(2):
-            quantize(zb_codes[:, b * BLOCK : (b + 1) * BLOCK], zb_scales[:, b * BLOCK : (b + 1) * BLOCK],
-                     zb_bf[:, b * BLOCK * PACK : (b + 1) * BLOCK * PACK])
+        vmax(z_bf[:, FIRST * PACK :].rearrange("p (b v t) -> p b v t", b=2, t=PACK)[:, :, :, 2:4],
+             zn[:, na:nb].rearrange("p b t v -> p b v t"), b2.rearrange("p t b v -> p b v t"))
+        quantize(z_codes[:, FIRST:T], z_scales[:, FIRST:T], z_bf[:, FIRST * PACK :])
         res = tile("last_out", [P, N // P, LAST], F32)
         for m in range(N // P):
-            mx(out_acc[2, m][:], *weights(1, m), zb_codes[:], zb_scales[:], False, True)
+            mx(out_acc[2, m][:], *weights(1, m), z_codes[:, FIRST:T], z_scales[:, FIRST:T], False, True)
         nc.scalar.activation(out=res[:, 0, :], in_=out_acc[2, 0][:], func=RELU)
         nc.vector.tensor_scalar(out=res[:, 1, :], in0=out_acc[2, 1][:], scalar1=0.0, scalar2=None, op0=MAX)
         nc.sync.dma_start(out=out[:, FIRST:T].rearrange("(m p) v -> p m v", p=P), in_=res[:])

@@ -85,15 +85,12 @@ def tile_picked_wsagecat_maxrelu_l_kernel(
                 in_=x_scales[:, 4 * q : 4 * q + 4, :].rearrange("g j c -> j g c").bitcast(I32),
             )
 
-        load_scales(0)
-        load_scales(1)
         load_w1(0, 0)
-        load_scales(2)
-        load_scales(3)
+        for q in range(4):
+            load_scales(q)
         load_w1(0, 1)
         for g in range(PASSES):
-            load_x(g, 0, HALF)
-            load_x(g, HALF, T)
+            load_x(g, 0, T)
         nc.sync.dma_start(offs[0][:], pos1)
         load_w1(1, 0)
         nc.sync.dma_start(offs[1][:], pos2)
@@ -195,7 +192,9 @@ def tile_picked_wsagecat_maxrelu_l_kernel(
         z01 = reuse.tile([P, 2, 2 * FIRST], BF16, name="z01", offset=0, align_bytes=ALIGN)[:, :, 0:T]
         for w in range(2):
             for t in range(2):
-                nc.sync.dma_start(out=h[w * HP : (w + 1) * HP, t * T : (t + 1) * T], in_=h[t * HP : (t + 1) * HP, h_cols(w)])
+                for c0, c1 in ([(0, T)], halves)[w]:
+                    nc.sync.dma_start(out=h[w * HP : (w + 1) * HP, t * T + c0 : t * T + c1],
+                                      in_=h[t * HP : (t + 1) * HP, h_cols(w, c0, c1)])
         for w in range(2):
             for t in range(2):
                 nc.sync.dma_start(out=z01[w * HP : (w + 1) * HP, t, :], in_=zm[t * HP : (t + 1) * HP, w, :])

@@ -89,8 +89,9 @@ def tile_picked_wsagecat_maxrelu_l_kernel(
         for q in range(4):
             load_scales(q)
         load_w1(0, 1)
-        for g in range(PASSES):
-            load_x(g, 0, T)
+        load_x(0, 0, T)
+        load_x(1, 0, HALF)
+        load_x(1, HALF, T)
         nc.sync.dma_start(offs[0][:], pos1)
         load_w1(1, 0)
         nc.sync.dma_start(offs[1][:], pos2)
@@ -117,9 +118,11 @@ def tile_picked_wsagecat_maxrelu_l_kernel(
         hi_codes = tile("hi_codes", [P, PASSES * P], U32)
         hi_scales = tile("hi_scales", [P, PASSES * P], U8)
         nat_bf = tile("nat_bf", [P, PASSES * 2 * K_PASS], BF16)
+        up_codes = tile("up_codes", [P, PASSES * P], U32)
+        up_scales = tile("up_scales", [P, PASSES * P], U8)
         nat_codes = tile("nat_codes", [P, PASSES * 2 * P], U32)
         nat_scales = tile("nat_scales", [P, PASSES * 2 * P], U8)
-        nat_view = nat_bf[:].rearrange("p (g t u a i j) -> p g u t a j i", g=PASSES, t=2, u=2, i=4, j=PACK)
+        nat_view = nat_bf[:].rearrange("p (u g t a i j) -> p g u t a j i", g=PASSES, t=2, u=2, i=4, j=PACK)
 
         for g in range(PASSES):
             nc.vector.tensor_copy(out=pair_view(lo_bf[g][:]), in_=raw_view(0, g)[:, 0])
@@ -130,8 +133,13 @@ def tile_picked_wsagecat_maxrelu_l_kernel(
                 nc.scalar.copy(out=nat_view[:, g, 0], in_=raw_view(0, g)[:, 1])
             quantize(lo_codes[:, g * P : (g + 1) * P], lo_scales[:, g * P : (g + 1) * P], lo_bf[g][:])
 
+        for g in range(PASSES):
+            for t in range(2):
+                col = (2 * g + t) * P
+                quantize(nat_codes[:, col : col + HP], nat_scales[:, col : col + HP], nat_bf[:, 2 * col : 2 * col + 2 * P])
+
         h = tile("h", [P, (PACK + 2) * T + SPARE], F32)
-        nc.gpsimd.memset(h[:, (PACK + 2) * T :], 0.0)
+        nc.vector.memset(h[:, (PACK + 2) * T :], 0.0)
         place = (5, 4, 2, 3)
 
         def h_cols(w, c0=0, c1=T):
@@ -163,19 +171,25 @@ def tile_picked_wsagecat_maxrelu_l_kernel(
 
         e = [tile("e%d" % d, [P, 2, 32, 32], BF16)[:, :, :, 0:16] for d in range(2)]
         gather(e[0][:, 0], 0, 0, 0, T)
-        gather(e[1][:, 0], 0, 1, 0, T)
-        for g in range(PASSES):
-            nc.scalar.copy(out=pair_view(hi_bf[:, g * K_PASS : (g + 1) * K_PASS]), in_=raw_view(1, g)[:, 0])
-        quantize(hi_codes[:], hi_scales[:], hi_bf[:])
-        for g in range(PASSES):
-            nc.scalar.copy(out=nat_view[:, g, 1], in_=raw_view(1, g)[:, 1])
-        late = hi_raw[:].bitcast(BF16).rearrange("p (w k r v) -> p k w r v", w=2, k=2, v=32)[:, :, :, :, 0:16]
+        late = hi_raw[:].bitcast(BF16).rearrange("p (w r k v) -> p k w r v", w=2, k=2, v=16)[:, :, :, 0:32]
         two = late[:, 0]
         third = late[:, 1]
-        vmax(two[:, 0], e[0][:, 0], e[1][:, 0])
-        gather(third[:, 0], 0, 2, 0, T)
+        for g in range(PASSES):
+            nc.scalar.copy(out=pair_view(hi_bf[:, g * K_PASS : (g + 1) * K_PASS]), in_=raw_view(1, g)[:, 0])
+            quantize(hi_codes[:, g * P : (g + 1) * P], hi_scales[:, g * P : (g + 1) * P],
+                     hi_bf[:, g * K_PASS : (g + 1) * K_PASS])
+            if g == 0:
+                gather(two[:, 1], 0, 1, 0, T)
+        for g in range(PASSES):
+            nc.scalar.copy(out=nat_view[:, g, 1], in_=raw_view(1, g)[:, 1])
+        vmax(two[:, 0], e[0][:, 0], two[:, 1])
         project(1, hi_codes, hi_scales, lambda g: g * P, halves, 2)
-        quantize(nat_codes[:], nat_scales[:], nat_bf[:])
+        quantize(up_codes[:], up_scales[:], nat_bf[:, PASSES * K_PASS :])
+        nc.sync.dma_start(out=nat_codes[:].bitcast(I32).rearrange("p (k u c) -> p u k c", u=2, c=HP)[:, 1],
+                          in_=up_codes[:].bitcast(I32).rearrange("p (k c) -> p k c", c=HP))
+        nc.sync.dma_start(out=nat_scales[:].bitcast(I32).rearrange("p (k u c) -> p u k c", u=2, c=HP // 4)[:, 1],
+                          in_=up_scales[:].bitcast(I32).rearrange("p (k c) -> p k c", c=HP // 4))
+        gather(third[:, 0], 0, 2, 0, T)
         gather(e[0][:, 1], 1, 0, 0, T)
         gather(e[1][:, 1], 1, 1, 0, T)
         gather(third[:, 1], 1, 2, 0, T)
@@ -192,9 +206,8 @@ def tile_picked_wsagecat_maxrelu_l_kernel(
         z01 = reuse.tile([P, 2, 2 * FIRST], BF16, name="z01", offset=0, align_bytes=ALIGN)[:, :, 0:T]
         for w in range(2):
             for t in range(2):
-                for c0, c1 in ([(0, T)], halves)[w]:
-                    nc.sync.dma_start(out=h[w * HP : (w + 1) * HP, t * T + c0 : t * T + c1],
-                                      in_=h[t * HP : (t + 1) * HP, h_cols(w, c0, c1)])
+                nc.sync.dma_start(out=h[w * HP : (w + 1) * HP, t * T : (t + 1) * T],
+                                  in_=h[t * HP : (t + 1) * HP, h_cols(w)])
         for w in range(2):
             for t in range(2):
                 nc.sync.dma_start(out=z01[w * HP : (w + 1) * HP, t, :], in_=zm[t * HP : (t + 1) * HP, w, :])
@@ -253,12 +266,15 @@ def tile_picked_wsagecat_maxrelu_l_kernel(
             quantize(z_codes[:, c0:c1], z_scales[:, c0:c1], z_bf[:, c0 * PACK : c1 * PACK])
             if i == 0:
                 gather(b2[:, i], 2 + i, 2, FIRST, T)
+            res = tile("first_out%d" % i, [P, N // P, c1 - c0], F32)
             for m in range(N // P):
-                res = tile("first_out%d%d" % (i, m), [P, c1 - c0], F32)
                 acc = out_acc[i, m]
                 mx(acc[:], *weights(1, m), z_codes[:, c0:c1], z_scales[:, c0:c1], False, True)
-                nc.scalar.activation(out=res[:], in_=acc[:], func=RELU)
-                nc.sync.dma_start(out=out[m * P : (m + 1) * P, c0:c1], in_=res[:])
+                nc.scalar.activation(out=res[:, m, :], in_=acc[:], func=RELU)
+                if i == 0:
+                    nc.sync.dma_start(out=out[m * P : (m + 1) * P, c0:c1], in_=res[:, m, :])
+            if i == 1:
+                nc.sync.dma_start(out=out[:, c0:c1].rearrange("(m p) v -> p m v", p=P), in_=res[:])
 
         vmax(z_bf[:, FIRST * PACK :].rearrange("p (b v t) -> p b v t", b=2, t=PACK)[:, :, :, 2:4],
              zn[:, na:nb].rearrange("p b t v -> p b v t"), b2.rearrange("p t b v -> p b v t"))

@@ -169,8 +169,8 @@ def tile_picked_wsagecat_maxrelu_l_kernel(
         def vmax(dst, one, other):
             nc.vector.tensor_tensor(out=dst, in0=one, in1=other, op=MAX)
 
-        e = [tile("e%d" % d, [P, 2, 32, 32], BF16)[:, :, :, 0:16] for d in range(2)]
-        gather(e[0][:, 0], 0, 0, 0, T)
+        e = tile("e", [P, 2, 32, 32], BF16)[:, :, :, 0:16]
+        gather(e[:, 0], 0, 0, 0, T)
         late = hi_raw[:].bitcast(BF16).rearrange("p (w r k v) -> p k w r v", w=2, k=2, v=16)[:, :, :, 0:32]
         two = late[:, 0]
         third = late[:, 1]
@@ -182,7 +182,7 @@ def tile_picked_wsagecat_maxrelu_l_kernel(
                 gather(two[:, 1], 0, 1, 0, T)
         for g in range(PASSES):
             nc.scalar.copy(out=nat_view[:, g, 1], in_=raw_view(1, g)[:, 1])
-        vmax(two[:, 0], e[0][:, 0], two[:, 1])
+        vmax(two[:, 0], e[:, 0], two[:, 1])
         project(1, hi_codes, hi_scales, lambda g: g * P, halves, 2)
         quantize(up_codes[:], up_scales[:], nat_bf[:, PASSES * K_PASS :])
         nc.sync.dma_start(out=nat_codes[:].bitcast(I32).rearrange("p (k u c) -> p u k c", u=2, c=HP)[:, 1],
@@ -190,27 +190,29 @@ def tile_picked_wsagecat_maxrelu_l_kernel(
         nc.sync.dma_start(out=nat_scales[:].bitcast(I32).rearrange("p (k u c) -> p u k c", u=2, c=HP // 4)[:, 1],
                           in_=up_scales[:].bitcast(I32).rearrange("p (k c) -> p k c", c=HP // 4))
         gather(third[:, 0], 0, 2, 0, T)
-        gather(e[0][:, 1], 1, 0, 0, T)
-        gather(e[1][:, 1], 1, 1, 0, T)
-        gather(third[:, 1], 1, 2, 0, T)
-        vmax(two[:, 1], e[0][:, 1], e[1][:, 1])
+        gather(two[:, 1], 1, 0, 0, T)
+        gather(third[:, 1], 1, 1, 0, T)
+        gather(e[:, 1], 1, 2, 0, T)
+        both = tile("both", [P, 2, T], BF16)
+        vmax(both[:].rearrange("p w (r v) -> p w r v", v=16), two, third)
         for w, groups in ((3, halves), (2, [(0, T)])):
             project(w, nat_codes, nat_scales, lambda g: (2 * g + w - 2) * P, groups, 4)
         nb = T // BLOCK
         na = FIRST // BLOCK
         f = [tile("f%d" % d, [P, nb, 2, BLOCK], BF16) for d in range(2)]
         gather(f[0][:, :, 1, :], 3, 0, 0, T)
-        zm = tile("zm", [P, 2, T], BF16, tag="x_codes0")
-        vmax(zm[:].rearrange("p w (r v) -> p w r v", v=16), two, third)
+        zm1 = tile("zm1", [P, T], BF16, tag="x_codes0")
+        vmax(zm1[:].rearrange("p (r v) -> p r v", v=16), both[:, 1].rearrange("p (r v) -> p r v", v=16), e[:, 1])
+        zm = (both[:, 0], zm1[:])
 
-        z01 = reuse.tile([P, 2, 2 * FIRST], BF16, name="z01", offset=0, align_bytes=ALIGN)[:, :, 0:T]
+        z01 = reuse.tile([P, 2, 2 * T], BF16, name="z01", offset=0, align_bytes=ALIGN)[:, :, 0:T]
         for w in range(2):
             for t in range(2):
                 nc.sync.dma_start(out=h[w * HP : (w + 1) * HP, t * T : (t + 1) * T],
                                   in_=h[t * HP : (t + 1) * HP, h_cols(w)])
         for w in range(2):
             for t in range(2):
-                nc.sync.dma_start(out=z01[w * HP : (w + 1) * HP, t, :], in_=zm[t * HP : (t + 1) * HP, w, :])
+                nc.sync.dma_start(out=z01[w * HP : (w + 1) * HP, t, :], in_=zm[w][t * HP : (t + 1) * HP])
 
         wh_bf = tile("wh_bf", [P, (2 * N + T) * PACK], BF16)
         for s in range(2):
@@ -235,13 +237,14 @@ def tile_picked_wsagecat_maxrelu_l_kernel(
             gather(f[1][:, :, t, :], 2 + t, 1, 0, T)
             gather(a2[:, :, t, :], 2 + t, 2, 0, FIRST)
             vmax(zn[:, :, t, :], zn[:, :, t, :], f[1][:, :, t, :])
-        za = reuse.tile([P, nb, 2, BLOCK], BF16, name="za", offset=0, align_bytes=ALIGN)
+        late_z = reuse.tile([P, 2 * na, 2, BLOCK], BF16, name="late_z", offset=0, align_bytes=ALIGN)
+        za = late_z[:, 2 : 2 + na]
         for t in (1, 0):
-            vmax(za[:, 0:na, t, :], zn[:, 0:na, t, :], a2[:, :, t, :])
+            vmax(za[:, :, t, :], zn[:, 0:na, t, :], a2[:, :, t, :])
         weave_blocks(z_bf[:, 0 : HALF * PACK], za[:, 0:4])
         weave_blocks(z_bf[:, HALF * PACK : FIRST * PACK], za[:, 4:na])
         wh_codes = tile("wh_codes", [P, 2 * N + T], U32)
-        wh_scales = reuse.tile([P, 2 * N + T], U8, name="wh_scales", offset=4 * T, align_bytes=ALIGN)
+        wh_scales = reuse.tile([P, 2 * N + T], U8, name="wh_scales", offset=6 * T, align_bytes=ALIGN)
         quantize(wh_codes[:], wh_scales[:], wh_bf[:])
 
         def weights(s, m):
@@ -259,13 +262,10 @@ def tile_picked_wsagecat_maxrelu_l_kernel(
 
         z_codes = tile("z_codes", [P, T], U32)
         z_scales = tile("z_scales", [P, T], U8)
-        b2 = za[:].rearrange("p (t b) s v -> p t b s v", t=2)[:, :, 0:2, 0, :]
+        b2 = late_z[:].rearrange("p (t b) s v -> p t b s v", t=2)[:, :, 0:2, 0, :]
         for i, (c0, c1) in enumerate(groups[:2]):
-            if i == 1:
-                gather(b2[:, i], 2 + i, 2, FIRST, T)
+            gather(b2[:, i], 2 + i, 2, FIRST, T)
             quantize(z_codes[:, c0:c1], z_scales[:, c0:c1], z_bf[:, c0 * PACK : c1 * PACK])
-            if i == 0:
-                gather(b2[:, i], 2 + i, 2, FIRST, T)
             res = tile("first_out%d" % i, [P, N // P, c1 - c0], F32)
             for m in range(N // P):
                 acc = out_acc[i, m]

@@ -15,6 +15,8 @@ FP8X4 = mybir.dt.float8_e4m3fn_x4
 RELU = mybir.ActivationFunctionType.Relu
 COPY = mybir.ActivationFunctionType.Copy
 MAX = mybir.AluOpType.max
+ADD = mybir.AluOpType.add
+SUB = mybir.AluOpType.subtract
 
 P = 128
 HP = P // 2
@@ -197,15 +199,14 @@ def tile_picked_wsagecat_maxrelu_l_kernel(
         vmax(both[:].rearrange("p w (r v) -> p w r v", v=16), two, third)
         for w, groups in ((3, halves), (2, [(0, T)])):
             project(w, nat_codes, nat_scales, lambda g: (2 * g + w - 2) * P, groups, 4)
-        nb = T // BLOCK
-        na = FIRST // BLOCK
-        f = [tile("f%d" % d, [P, nb, 2, BLOCK], BF16) for d in range(2)]
-        gather(f[0][:, :, 1, :], 3, 0, 0, T)
+        zn = tile("zn", [P, 2, 4, P + GAP], BF16)[:, :, :, 0:P]
+        second = tile("second", [P, 2, 4, P + GAP], BF16)[:, :, :, 0:P]
+        gather(zn[:, 1], 3, 0, 0, T)
         zm1 = tile("zm1", [P, T], BF16, tag="x_codes0")
         vmax(zm1[:].rearrange("p (r v) -> p r v", v=16), both[:, 1].rearrange("p (r v) -> p r v", v=16), e[:, 1])
         zm = (both[:, 0], zm1[:])
 
-        z01 = reuse.tile([P, 2, 2 * T], BF16, name="z01", offset=0, align_bytes=ALIGN)[:, :, 0:T]
+        z01 = reuse.tile([P, 2, 3 * T], BF16, name="z01", offset=0, align_bytes=ALIGN)[:, :, 0:T]
         for w in range(2):
             for t in range(2):
                 nc.sync.dma_start(out=h[w * HP : (w + 1) * HP, t * T : (t + 1) * T],
@@ -220,38 +221,40 @@ def tile_picked_wsagecat_maxrelu_l_kernel(
                            in_=w23_raw[:, s].rearrange("p t (c i) -> p c t i", i=4))
         nc.scalar.copy(out=wh_bf[:, 2 * N * PACK :].rearrange("p (c i t) -> p c t i", i=4, t=PACK),
                        in_=h[:, 0 : PACK * T].rearrange("p (t c i) -> p c t i", t=PACK, i=4))
-        z_bf = h[:, 0 : 2 * T].bitcast(BF16)
+        z_bf = tile("z_bf", [P, T * PACK], BF16)[:]
         nc.scalar.copy(out=z_bf.rearrange("p (c i t) -> p c t i", i=4, t=PACK)[:, :, 0:2, :],
                        in_=z01.rearrange("p t (c i) -> p c t i", i=4))
 
-        def weave_blocks(dst, pair):
+        a2 = tile("a2", [P, 2, 3, P + GAP], BF16)[:, :, :, 0:P]
+        gather(second[:, 1], 3, 1, 0, T)
+        diff = tile("diff", [P, FIRST], F32)
+        gain = h[:, 0:FIRST]
+        nc.gpsimd.tensor_tensor(out=diff[:].rearrange("p (b v) -> p b v", v=P), in0=zn[:, 1, 1:4], in1=second[:, 1, 1:4], op=SUB)
+        nc.scalar.activation(out=gain, in_=diff[:], func=RELU)
+        nc.gpsimd.tensor_tensor(out=zn[:, 1, 1:4], in0=gain.rearrange("p (b v) -> p b v", v=P), in1=second[:, 1, 1:4], op=ADD)
+        gather(a2[:, 1], 3, 2, LAST, T)
+        gather(zn[:, 0], 2, 0, 0, T)
+        gather(second[:, 0], 2, 1, 0, T)
+        gather(a2[:, 0], 2, 2, LAST, T)
+        five = zn.rearrange("p t b v -> p (t b) v")[:, 0:5]
+        vmax(five, five, second.rearrange("p t b v -> p (t b) v")[:, 0:5])
+        late_z = reuse.tile([P, 2, 2, T], BF16, name="late_z", offset=0, align_bytes=ALIGN)
+        za = late_z[:, 0]
+        for t in (1, 0):
+            vmax(za[:, t, LAST:T].rearrange("p (b v) -> p b v", v=P), zn[:, t, 1:4], a2[:, t])
+        for c0, c1 in ((LAST, FIRST), (FIRST, T)):
             nc.scalar.copy(
-                out=dst.rearrange("p (b c i t) -> p b c t i", c=BLOCK // 4, i=4, t=PACK)[:, :, :, 2:4, :],
-                in_=pair.rearrange("p b t (c i) -> p b c t i", i=4))
-
-        a2 = tile("a2", [P, na, 2, BLOCK], BF16)
-        zn = f[0]
-        for t in (1, 0):
-            if t == 0:
-                gather(f[0][:, :, t, :], 2 + t, 0, 0, T)
-            gather(f[1][:, :, t, :], 2 + t, 1, 0, T)
-            gather(a2[:, :, t, :], 2 + t, 2, 0, FIRST)
-            vmax(zn[:, :, t, :], zn[:, :, t, :], f[1][:, :, t, :])
-        late_z = reuse.tile([P, 2 * na, 2, BLOCK], BF16, name="late_z", offset=0, align_bytes=ALIGN)
-        za = late_z[:, 2 : 2 + na]
-        for t in (1, 0):
-            vmax(za[:, :, t, :], zn[:, 0:na, t, :], a2[:, :, t, :])
-        weave_blocks(z_bf[:, 0 : HALF * PACK], za[:, 0:4])
-        weave_blocks(z_bf[:, HALF * PACK : FIRST * PACK], za[:, 4:na])
+                out=z_bf[:, c0 * PACK : c1 * PACK].rearrange("p (c i t) -> p c t i", i=4, t=PACK)[:, :, 2:4, :],
+                in_=za[:, :, c0:c1].rearrange("p t (c i) -> p c t i", i=4))
         wh_codes = tile("wh_codes", [P, 2 * N + T], U32)
-        wh_scales = reuse.tile([P, 2 * N + T], U8, name="wh_scales", offset=6 * T, align_bytes=ALIGN)
+        wh_scales = reuse.tile([P, 2 * N + T], U8, name="wh_scales", offset=8 * T, align_bytes=ALIGN)
         quantize(wh_codes[:], wh_scales[:], wh_bf[:])
 
         def weights(s, m):
             cols = slice(s * N + m * P, s * N + (m + 1) * P)
             return wh_codes[:, cols], wh_scales[:, cols]
 
-        groups = [(0, HALF), (HALF, FIRST), (FIRST, T)]
+        groups = [(LAST, FIRST), (FIRST, T), (0, LAST)]
         banks = (0, 1, 2, 3, 6, 7)
         out_acc = {}
         for i, (c0, c1) in enumerate(groups):
@@ -262,9 +265,9 @@ def tile_picked_wsagecat_maxrelu_l_kernel(
 
         z_codes = tile("z_codes", [P, T], U32)
         z_scales = tile("z_scales", [P, T], U8)
-        b2 = late_z[:].rearrange("p (t b) s v -> p t b s v", t=2)[:, :, 0:2, 0, :]
+        b2 = za.rearrange("p b (t v) -> p t b v", t=2)[:, :, :, 0:BLOCK]
         for i, (c0, c1) in enumerate(groups[:2]):
-            gather(b2[:, i], 2 + i, 2, FIRST, T)
+            gather(b2[:, i], 2 + i, 2, 0, LAST)
             quantize(z_codes[:, c0:c1], z_scales[:, c0:c1], z_bf[:, c0 * PACK : c1 * PACK])
             res = tile("first_out%d" % i, [P, N // P, c1 - c0], F32)
             for m in range(N // P):
@@ -276,12 +279,12 @@ def tile_picked_wsagecat_maxrelu_l_kernel(
             if i == 1:
                 nc.sync.dma_start(out=out[:, c0:c1].rearrange("(m p) v -> p m v", p=P), in_=res[:])
 
-        vmax(z_bf[:, FIRST * PACK :].rearrange("p (b v t) -> p b v t", b=2, t=PACK)[:, :, :, 2:4],
-             zn[:, na:nb].rearrange("p b t v -> p b v t"), b2.rearrange("p t b v -> p b v t"))
-        quantize(z_codes[:, FIRST:T], z_scales[:, FIRST:T], z_bf[:, FIRST * PACK :])
+        vmax(z_bf[:, 0 : LAST * PACK].rearrange("p (b v t) -> p b v t", b=2, t=PACK)[:, :, :, 2:4],
+             zn[:, :, 0].rearrange("p t (b v) -> p b v t", b=2), b2.rearrange("p t b v -> p b v t"))
+        quantize(z_codes[:, 0:LAST], z_scales[:, 0:LAST], z_bf[:, 0 : LAST * PACK])
         res = tile("last_out", [P, N // P, LAST], F32)
         for m in range(N // P):
-            mx(out_acc[2, m][:], *weights(1, m), z_codes[:, FIRST:T], z_scales[:, FIRST:T], False, True)
+            mx(out_acc[2, m][:], *weights(1, m), z_codes[:, 0:LAST], z_scales[:, 0:LAST], False, True)
         nc.scalar.activation(out=res[:, 0, :], in_=out_acc[2, 0][:], func=RELU)
         nc.vector.tensor_scalar(out=res[:, 1, :], in0=out_acc[2, 1][:], scalar1=0.0, scalar2=None, op0=MAX)
-        nc.sync.dma_start(out=out[:, FIRST:T].rearrange("(m p) v -> p m v", p=P), in_=res[:])
+        nc.sync.dma_start(out=out[:, 0:LAST].rearrange("(m p) v -> p m v", p=P), in_=res[:])

@@ -191,12 +191,23 @@ def tile_picked_wsagecat_maxrelu_l_kernel(
                           in_=up_codes[:].bitcast(I32).rearrange("p (k c) -> p k c", c=HP))
         nc.sync.dma_start(out=nat_scales[:].bitcast(I32).rearrange("p (k u c) -> p u k c", u=2, c=HP // 4)[:, 1],
                           in_=up_scales[:].bitcast(I32).rearrange("p (k c) -> p k c", c=HP // 4))
+        wh_bf = tile("wh_bf", [P, (2 * N + T) * PACK], BF16, tag="nat_bf")
+        nc.gpsimd.tensor_scalar(out=wh_bf[:, 0 : N * PACK].rearrange("p (c t) -> p c t", t=PACK),
+                                in0=w23_raw[:, 0].rearrange("p t c -> p c t"),
+                                scalar1=1.0, scalar2=0.0, op0=mybir.AluOpType.mult, op1=ADD)
+        nc.scalar.copy(out=wh_bf[:, N * PACK : 2 * N * PACK].rearrange("p (c i t) -> p c t i", i=4, t=PACK),
+                       in_=w23_raw[:, 1].rearrange("p t (c i) -> p c t i", i=4))
         gather(third[:, 0], 0, 2, 0, T)
+        both = tile("both", [P, 2, T], BF16)
+        diff0 = tile("diff0", [P, T], F32)
+        nc.gpsimd.tensor_tensor(out=diff0[:].rearrange("p (r v) -> p r v", v=16), in0=two[:, 0], in1=third[:, 0], op=SUB)
+        nc.scalar.activation(out=diff0[:], in_=diff0[:], func=RELU)
+        nc.gpsimd.tensor_tensor(out=both[:, 0].rearrange("p (r v) -> p r v", v=16),
+                                in0=diff0[:].rearrange("p (r v) -> p r v", v=16), in1=third[:, 0], op=ADD)
         gather(two[:, 1], 1, 0, 0, T)
         gather(third[:, 1], 1, 1, 0, T)
         gather(e[:, 1], 1, 2, 0, T)
-        both = tile("both", [P, 2, T], BF16)
-        vmax(both[:].rearrange("p w (r v) -> p w r v", v=16), two, third)
+        vmax(both[:, 1].rearrange("p (r v) -> p r v", v=16), two[:, 1], third[:, 1])
         for w, groups in ((3, halves), (2, [(0, T)])):
             project(w, nat_codes, nat_scales, lambda g: (2 * g + w - 2) * P, groups, 4)
         zn = tile("zn", [P, 2, 4, P + GAP], BF16)[:, :, :, 0:P]
@@ -215,10 +226,6 @@ def tile_picked_wsagecat_maxrelu_l_kernel(
             for t in range(2):
                 nc.sync.dma_start(out=z01[w * HP : (w + 1) * HP, t, :], in_=zm[w][t * HP : (t + 1) * HP])
 
-        wh_bf = tile("wh_bf", [P, (2 * N + T) * PACK], BF16)
-        for s in range(2):
-            nc.scalar.copy(out=wh_bf[:, s * N * PACK : (s + 1) * N * PACK].rearrange("p (c i t) -> p c t i", i=4, t=PACK),
-                           in_=w23_raw[:, s].rearrange("p t (c i) -> p c t i", i=4))
         nc.scalar.copy(out=wh_bf[:, 2 * N * PACK :].rearrange("p (c i t) -> p c t i", i=4, t=PACK),
                        in_=h[:, 0 : PACK * T].rearrange("p (t c i) -> p c t i", t=PACK, i=4))
         z_bf = tile("z_bf", [P, T * PACK], BF16)[:]

@@ -108,10 +108,10 @@ def tile_picked_wsagecat_maxrelu_l_kernel(
                 )
 
         def raw_view(u, g):
-            return w1_raw[u, g].rearrange("p (j a v i e) -> p v e a j i", j=PACK, v=2, i=4, e=2)
+            return w1_raw[u, g].rearrange("p (j a v i e) -> p v a j i e", j=PACK, v=2, i=4, e=2)
 
         def pair_view(values):
-            return values.rearrange("p (t a i j) -> p t a j i", t=2, i=4, j=PACK)
+            return values.rearrange("p (t a i j) -> p a j i t", t=2, i=4, j=PACK)
 
         lo_bf = [tile("lo_bf%d" % g, [P, K_PASS], BF16) for g in range(PASSES)]
         lo_scales = tile("lo_scales", [P, PASSES * P], U8)
@@ -124,13 +124,13 @@ def tile_picked_wsagecat_maxrelu_l_kernel(
         up_scales = tile("up_scales", [P, PASSES * P], U8)
         nat_codes = tile("nat_codes", [P, PASSES * 2 * P], U32)
         nat_scales = tile("nat_scales", [P, PASSES * 2 * P], U8)
-        nat_view = nat_bf[:].rearrange("p (u g t a i j) -> p g u t a j i", g=PASSES, t=2, u=2, i=4, j=PACK)
+        nat_view = nat_bf[:].rearrange("p (u g t a i j) -> p g u a j i t", g=PASSES, t=2, u=2, i=4, j=PACK)
 
         for g in range(PASSES):
             nc.vector.tensor_copy(out=pair_view(lo_bf[g][:]), in_=raw_view(0, g)[:, 0])
             if g == 0:
                 for t in range(2):
-                    nc.scalar.activation(out=nat_view[:, g, 0, t], in_=raw_view(0, g)[:, 1, t], func=COPY)
+                    nc.scalar.activation(out=nat_view[:, g, 0, :, :, :, t], in_=raw_view(0, g)[:, 1, :, :, :, t], func=COPY)
             else:
                 nc.scalar.copy(out=nat_view[:, g, 0], in_=raw_view(0, g)[:, 1])
             quantize(lo_codes[:, g * P : (g + 1) * P], lo_scales[:, g * P : (g + 1) * P], lo_bf[g][:])

@@ -91,7 +91,8 @@ def tile_picked_wsagecat_maxrelu_l_kernel(
         for q in range(4):
             load_scales(q)
         load_w1(0, 1)
-        load_x(0, 0, T)
+        load_x(0, 0, HALF)
+        load_x(0, HALF, T)
         load_x(1, 0, HALF)
         load_x(1, HALF, T)
         nc.sync.dma_start(offs[0][:], pos1)
@@ -140,12 +141,15 @@ def tile_picked_wsagecat_maxrelu_l_kernel(
                 col = (2 * g + t) * P
                 quantize(nat_codes[:, col : col + HP], nat_scales[:, col : col + HP], nat_bf[:, 2 * col : 2 * col + 2 * P])
 
-        h = tile("h", [P, (PACK + 2) * T + SPARE], F32)
-        nc.vector.memset(h[:, (PACK + 2) * T :], 0.0)
-        place = (5, 4, 2, 3)
+        pitch = T + SPARE
+        h = tile("h", [P, (PACK + 1) * pitch], F32)
+        slots = h[:].rearrange("p (s c) -> p s c", c=pitch)
+        nc.vector.memset(slots[:, 0:1, T:], 0.0)
+        nc.vector.memset(slots[:, 2:, T:], 0.0)
+        place = (0, 4, 2, 3)
 
         def h_cols(w, c0=0, c1=T):
-            return slice(place[w] * T + c0, place[w] * T + c1)
+            return slice(place[w] * pitch + c0, place[w] * pitch + c1)
 
         def project(w, codes, scales, col, groups, bank):
             accs = [ps.tile([P, c1 - c0], F32, name="h_acc%d%d" % (w, i), tag="bank%d" % (bank + i))
@@ -219,15 +223,15 @@ def tile_picked_wsagecat_maxrelu_l_kernel(
 
         z01 = reuse.tile([P, 2, 3 * T], BF16, name="z01", offset=0, align_bytes=ALIGN)[:, :, 0:T]
         for w in range(2):
-            for t in range(2):
-                nc.sync.dma_start(out=h[w * HP : (w + 1) * HP, t * T : (t + 1) * T],
+            for t in range(1 - w, 2):
+                nc.sync.dma_start(out=slots[w * HP : (w + 1) * HP, t, 0:T],
                                   in_=h[t * HP : (t + 1) * HP, h_cols(w)])
         for w in range(2):
             for t in range(2):
                 nc.sync.dma_start(out=z01[w * HP : (w + 1) * HP, t, :], in_=zm[w][t * HP : (t + 1) * HP])
 
         nc.scalar.copy(out=wh_bf[:, 2 * N * PACK :].rearrange("p (c i t) -> p c t i", i=4, t=PACK),
-                       in_=h[:, 0 : PACK * T].rearrange("p (t c i) -> p c t i", t=PACK, i=4))
+                       in_=slots[:, 0:PACK, 0:T].rearrange("p t (c i) -> p c t i", i=4))
         z_bf = tile("z_bf", [P, T * PACK], BF16)[:]
         nc.scalar.copy(out=z_bf.rearrange("p (c i t) -> p c t i", i=4, t=PACK)[:, :, 0:2, :],
                        in_=z01.rearrange("p t (c i) -> p c t i", i=4))
@@ -235,7 +239,7 @@ def tile_picked_wsagecat_maxrelu_l_kernel(
         a2 = tile("a2", [P, 2, 3, P + GAP], BF16)[:, :, :, 0:P]
         gather(second[:, 1], 3, 1, 0, T)
         diff = tile("diff", [P, FIRST], F32)
-        gain = h[:, 0:FIRST]
+        gain = slots[:, 1, 0:FIRST]
         nc.gpsimd.tensor_tensor(out=diff[:].rearrange("p (b v) -> p b v", v=P), in0=zn[:, 1, 1:4], in1=second[:, 1, 1:4], op=SUB)
         nc.scalar.activation(out=gain, in_=diff[:], func=RELU)
         nc.gpsimd.tensor_tensor(out=zn[:, 1, 1:4], in0=gain.rearrange("p (b v) -> p b v", v=P), in1=second[:, 1, 1:4], op=ADD)

@@ -196,10 +196,10 @@ def tile_picked_wsagecat_maxrelu_l_kernel(
         nc.sync.dma_start(out=nat_scales[:].bitcast(I32).rearrange("p (k u c) -> p u k c", u=2, c=HP // 4)[:, 1],
                           in_=up_scales[:].bitcast(I32).rearrange("p (k c) -> p k c", c=HP // 4))
         wh_bf = tile("wh_bf", [P, (2 * N + T) * PACK], BF16, tag="nat_bf")
-        nc.gpsimd.tensor_scalar(out=wh_bf[:, 0 : N * PACK].rearrange("p (c t) -> p c t", t=PACK),
+        nc.gpsimd.tensor_scalar(out=wh_bf[:, (N + T) * PACK :].rearrange("p (c t) -> p c t", t=PACK),
                                 in0=w23_raw[:, 0].rearrange("p t c -> p c t"),
                                 scalar1=1.0, scalar2=0.0, op0=mybir.AluOpType.mult, op1=ADD)
-        nc.scalar.copy(out=wh_bf[:, N * PACK : 2 * N * PACK].rearrange("p (c i t) -> p c t i", i=4, t=PACK),
+        nc.scalar.copy(out=wh_bf[:, 0 : N * PACK].rearrange("p (c i t) -> p c t i", i=4, t=PACK),
                        in_=w23_raw[:, 1].rearrange("p t (c i) -> p c t i", i=4))
         gather(third[:, 0], 0, 2, 0, T)
         both = tile("both", [P, 2, T], BF16)
@@ -230,7 +230,7 @@ def tile_picked_wsagecat_maxrelu_l_kernel(
             for t in range(2):
                 nc.sync.dma_start(out=z01[w * HP : (w + 1) * HP, t, :], in_=zm[w][t * HP : (t + 1) * HP])
 
-        nc.scalar.copy(out=wh_bf[:, 2 * N * PACK :].rearrange("p (c i t) -> p c t i", i=4, t=PACK),
+        nc.scalar.copy(out=wh_bf[:, N * PACK : (N + T) * PACK].rearrange("p (c i t) -> p c t i", i=4, t=PACK),
                        in_=slots[:, 0:PACK, 0:T].rearrange("p t (c i) -> p c t i", i=4))
         z_bf = tile("z_bf", [P, T * PACK], BF16)[:]
         nc.scalar.copy(out=z_bf.rearrange("p (c i t) -> p c t i", i=4, t=PACK)[:, :, 0:2, :],
@@ -253,26 +253,31 @@ def tile_picked_wsagecat_maxrelu_l_kernel(
         za = late_z[:, 0]
         for t in (1, 0):
             vmax(za[:, t, LAST:T].rearrange("p (b v) -> p b v", v=P), zn[:, t, 1:4], a2[:, t])
-        for c0, c1 in ((LAST, FIRST), (FIRST, T)):
+        for c0, c1 in ((HALF, T), (LAST, HALF)):
             nc.scalar.copy(
                 out=z_bf[:, c0 * PACK : c1 * PACK].rearrange("p (c i t) -> p c t i", i=4, t=PACK)[:, :, 2:4, :],
                 in_=za[:, :, c0:c1].rearrange("p t (c i) -> p c t i", i=4))
         wh_codes = tile("wh_codes", [P, 2 * N + T], U32)
         wh_scales = reuse.tile([P, 2 * N + T], U8, name="wh_scales", offset=8 * T, align_bytes=ALIGN)
-        quantize(wh_codes[:], wh_scales[:], wh_bf[:])
+        for c0 in (T, 0):
+            quantize(wh_codes[:, c0 : c0 + T], wh_scales[:, c0 : c0 + T], wh_bf[:, c0 * PACK : (c0 + T) * PACK])
 
         def weights(s, m):
-            cols = slice(s * N + m * P, s * N + (m + 1) * P)
+            cols = slice((1 - s) * (N + T) + m * P, (1 - s) * (N + T) + (m + 1) * P)
             return wh_codes[:, cols], wh_scales[:, cols]
 
-        groups = [(LAST, FIRST), (FIRST, T), (0, LAST)]
+        groups = [(HALF, T), (LAST, HALF), (0, LAST)]
         banks = (0, 1, 2, 3, 6, 7)
         out_acc = {}
         for i, (c0, c1) in enumerate(groups):
             for m in range(N // P):
                 acc = ps.tile([P, c1 - c0], F32, name="out_acc%d%d" % (i, m), tag="bank%d" % banks[2 * i + m])
-                mx(acc[:], *weights(0, m), wh_codes[:, 2 * N + c0 : 2 * N + c1], wh_scales[:, 2 * N + c0 : 2 * N + c1], True, False)
+                mx(acc[:], *weights(0, m), wh_codes[:, N + c0 : N + c1], wh_scales[:, N + c0 : N + c1], True, False)
                 out_acc[i, m] = acc
+            if i == 0:
+                for m in range(N // P):
+                    idle = ps.tile([P, T], F32, name="idle%d" % m, tag="bank%d" % (4 + m))
+                    mx(idle[:], *weights(0, m), x_codes[1][:], x_planes[:, 1, :], True, True)
 
         z_codes = tile("z_codes", [P, T], U32)
         z_scales = tile("z_scales", [P, T], U8)

@@ -165,7 +165,7 @@ def tile_picked_wsagecat_maxrelu_l_kernel(
                         nc.scalar.activation(out=h[:, h_cols(w, c0, c1)], in_=acc[:], func=RELU)
 
         halves = [(0, HALF), (HALF, T)]
-        project(0, lo_codes, lo_scales, lambda g: g * P, halves, 0)
+        project(0, lo_codes, lo_scales, lambda g: g * P, [(0, HALF), (HALF, FIRST), (FIRST, T)], 5)
 
         def gather(dst, w, d, v0, v1):
             width = T + SPARE if v1 - v0 == T else T
@@ -259,8 +259,9 @@ def tile_picked_wsagecat_maxrelu_l_kernel(
                 in_=za[:, :, c0:c1].rearrange("p t (c i) -> p c t i", i=4))
         wh_codes = tile("wh_codes", [P, 2 * N + T], U32)
         wh_scales = reuse.tile([P, 2 * N + T], U8, name="wh_scales", offset=8 * T, align_bytes=ALIGN)
-        for c0 in (T, 0):
-            quantize(wh_codes[:, c0 : c0 + T], wh_scales[:, c0 : c0 + T], wh_bf[:, c0 * PACK : (c0 + T) * PACK])
+
+        def quantize_wh(c0, c1):
+            quantize(wh_codes[:, c0:c1], wh_scales[:, c0:c1], wh_bf[:, c0 * PACK : c1 * PACK])
 
         def weights(s, m):
             cols = slice((1 - s) * (N + T) + m * P, (1 - s) * (N + T) + (m + 1) * P)
@@ -269,38 +270,51 @@ def tile_picked_wsagecat_maxrelu_l_kernel(
         groups = [(HALF, T), (LAST, HALF), (0, LAST)]
         banks = (0, 1, 2, 3, 6, 7)
         out_acc = {}
-        for i, (c0, c1) in enumerate(groups):
+        z_codes = tile("z_codes", [P, T], U32)
+        z_scales = tile("z_scales", [P, T], U8)
+
+        def open_group(i):
+            c0, c1 = groups[i]
             for m in range(N // P):
                 acc = ps.tile([P, c1 - c0], F32, name="out_acc%d%d" % (i, m), tag="bank%d" % banks[2 * i + m])
                 mx(acc[:], *weights(0, m), wh_codes[:, N + c0 : N + c1], wh_scales[:, N + c0 : N + c1], True, False)
                 out_acc[i, m] = acc
-            if i == 0:
-                for m in range(N // P):
-                    idle = ps.tile([P, T], F32, name="idle%d" % m, tag="bank%d" % (4 + m))
-                    mx(idle[:], *weights(0, m), x_codes[1][:], x_planes[:, 1, :], True, True)
 
-        z_codes = tile("z_codes", [P, T], U32)
-        z_scales = tile("z_scales", [P, T], U8)
-        b2 = za.rearrange("p b (t v) -> p t b v", t=2)[:, :, :, 0:BLOCK]
-        for i, (c0, c1) in enumerate(groups[:2]):
-            gather(b2[:, i], 2 + i, 2, 0, LAST)
+        def quantize_z(i):
+            c0, c1 = groups[i]
             quantize(z_codes[:, c0:c1], z_scales[:, c0:c1], z_bf[:, c0 * PACK : c1 * PACK])
-            res = tile("first_out%d" % i, [P, N // P, c1 - c0], F32)
-            for m in range(N // P):
-                acc = out_acc[i, m]
-                mx(acc[:], *weights(1, m), z_codes[:, c0:c1], z_scales[:, c0:c1], False, True)
-                nc.scalar.activation(out=res[:, m, :], in_=acc[:], func=RELU)
-                if i == 0:
-                    nc.sync.dma_start(out=out[m * P : (m + 1) * P, c0:c1], in_=res[:, m, :])
-            if i == 1:
-                nc.sync.dma_start(out=out[:, c0:c1].rearrange("(m p) v -> p m v", p=P), in_=res[:])
 
+        def close_group(i, m):
+            c0, c1 = groups[i]
+            mx(out_acc[i, m][:], *weights(1, m), z_codes[:, c0:c1], z_scales[:, c0:c1], False, True)
+
+        b2 = za.rearrange("p b (t v) -> p t b v", t=2)[:, :, :, 0:BLOCK]
+        quantize_wh(T, 2 * T)
+        quantize_wh(0, N)
+        open_group(0)
+        gather(b2[:, 0], 2, 2, 0, LAST)
+        quantize_z(0)
+        res = tile("first_out", [P, N // P, HALF], F32)
+        for m in range(N // P):
+            close_group(0, m)
+            nc.scalar.activation(out=res[:, m, :], in_=out_acc[0, m][:], func=RELU)
+            nc.sync.dma_start(out=out[m * P : (m + 1) * P, HALF:T], in_=res[:, m, :])
+        gather(b2[:, 1], 3, 2, 0, LAST)
+        quantize_wh(N, T)
+        open_group(1)
+        open_group(2)
         vmax(z_bf[:, 0 : LAST * PACK].rearrange("p (b v t) -> p b v t", b=2, t=PACK)[:, :, :, 2:4],
              zn[:, :, 0].rearrange("p t (b v) -> p b v t", b=2), b2.rearrange("p t b v -> p b v t"))
-        quantize(z_codes[:, 0:LAST], z_scales[:, 0:LAST], z_bf[:, 0 : LAST * PACK])
+        quantize_z(1)
+        quantize_z(2)
+        res = tile("second_out", [P, N // P, LAST], F32)
+        for m in range(N // P):
+            close_group(1, m)
+            nc.scalar.activation(out=res[:, m, :], in_=out_acc[1, m][:], func=RELU)
+        nc.sync.dma_start(out=out[:, LAST:HALF].rearrange("(m p) v -> p m v", p=P), in_=res[:])
         res = tile("last_out", [P, N // P, LAST], F32)
         for m in range(N // P):
-            mx(out_acc[2, m][:], *weights(1, m), z_codes[:, 0:LAST], z_scales[:, 0:LAST], False, True)
+            close_group(2, m)
         nc.scalar.activation(out=res[:, 0, :], in_=out_acc[2, 0][:], func=RELU)
         nc.vector.tensor_scalar(out=res[:, 1, :], in0=out_acc[2, 1][:], scalar1=0.0, scalar2=None, op0=MAX)
         nc.sync.dma_start(out=out[:, 0:LAST].rearrange("(m p) v -> p m v", p=P), in_=res[:])

from contextlib import ExitStack

import concourse.mybir as mybir

K, T, H, N = 1024, 512, 512, 256
FLOPS = 2 * K * H * T + 2 * 2 * H * N * T

F32 = mybir.dt.float32
BF16 = mybir.dt.bfloat16
I32 = mybir.dt.int32
U32 = mybir.dt.uint32
U16 = mybir.dt.uint16
U8 = mybir.dt.uint8
FP8X4 = mybir.dt.float8_e4m3fn_x4
RELU = mybir.ActivationFunctionType.Relu
COPY = mybir.ActivationFunctionType.Copy
MAX = mybir.AluOpType.max
ADD = mybir.AluOpType.add
SUB = mybir.AluOpType.subtract

P = 128
HP = P // 2
PACK = 4
K_PASS = P * PACK
PASSES = K // K_PASS
HALF = T // 2
FIRST = 384
LAST = T - FIRST
ALIGN = 64
SPARE = 192
BLOCK = 64
GAP = 32


def tile_picked_wsagecat_maxrelu_l_kernel(
    tc, x_words, x_scales, w1, w2, w3, pos1, pos2, pos3, out
):
    nc = tc.nc
    with ExitStack() as ctx:
        lists = ctx.enter_context(tc.tile_pool(name="lists", bufs=1))
        sb = ctx.enter_context(tc.tile_pool(name="sb", bufs=1))
        reuse = ctx.enter_context(tc.tile_pool(name="reuse", bufs=1))
        ps = ctx.enter_context(tc.psum_pool(name="ps", bufs=1))

        def tile(name, shape, dtype, tag=None):
            return sb.tile(shape, dtype, name=name, tag=tag or name, align_bytes=ALIGN)

        def quantize(codes, scales, values):
            nc.vector.quantize_mx(out=codes.bitcast(FP8X4), scales=scales, in_=values)

        def mx(acc, lhs_codes, lhs_scales, rhs_codes, rhs_scales, start, stop):
            nc.tensor.matmul_mx(
                out=acc,
                lhsT=lhs_codes.bitcast(FP8X4),
                lhsT_scale=lhs_scales,
                rhs=rhs_codes.bitcast(FP8X4),
                rhs_scale=rhs_scales,
                start=start,
                stop=stop,
            )

        x_planes = tile("x_planes", [P, PASSES, T], U8)
        raw_cols = PACK * H // 2
        w1_raw = {(0, g): tile("w1_raw0%d" % g, [P, raw_cols], F32)[:] for g in range(PASSES)}
        hi_raw = tile("hi_raw", [P, PASSES * raw_cols], F32)
        for g in range(PASSES):
            w1_raw[1, g] = hi_raw[:, (1 - g) * raw_cols : (2 - g) * raw_cols]
        x_codes = [tile("x_codes%d" % g, [P, T], U32) for g in range(PASSES)]
        offs = [lists.tile([P, T // 16], U16, name="list%d" % d, tag="list%d" % d) for d in range(3)]

        def load_w1(u, g):
            nc.sync.dma_start(
                out=w1_raw[u, g].rearrange("p (j c) -> p j c", j=PACK),
                in_=w1[g * K_PASS : (g + 1) * K_PASS, u * (H // 2) : (u + 1) * (H // 2)].rearrange(
                    "(p j) c -> p j c", j=PACK),
            )

        def load_x(g, c0, c1):
            nc.sync.dma_start(
                out=x_codes[g][:, c0:c1].bitcast(I32),
                in_=x_words[g].rearrange("p n t -> p (n t)")[:, c0 * PACK : c1 * PACK].bitcast(I32),
            )

        def load_scales(q):
            nc.sync.dma_start(
                out=x_planes[32 * q : 32 * q + 4].bitcast(I32),
                in_=x_scales[:, 4 * q : 4 * q + 4, :].rearrange("g j c -> j g c").bitcast(I32),
            )

        load_w1(0, 0)
        for q in range(4):
            load_scales(q)
        load_w1(0, 1)
        load_x(0, 0, HALF)
        load_x(0, HALF, T)
        load_x(1, 0, HALF)
        load_x(1, HALF, T)
        nc.sync.dma_start(offs[0][:], pos1)
        load_w1(1, 0)
        nc.sync.dma_start(offs[1][:], pos2)
        load_w1(1, 1)
        nc.sync.dma_start(offs[2][:], pos3)
        w23_raw = tile("w23_raw", [P, 2, PACK, N], F32)
        for s, w in enumerate((w2, w3)):
            for u in range(2):
                nc.sync.dma_start(
                    out=w23_raw[:, s, 2 * u : 2 * u + 2, :].rearrange("p e n -> p (e n)"),
                    in_=w.rearrange("(a u i e) n -> u a i (e n)", u=2, i=4, e=2)[u],
                )

        def raw_view(u, g):
            return w1_raw[u, g].rearrange("p (j a v i e) -> p v a j i e", j=PACK, v=2, i=4, e=2)

        def pair_view(values):
            return values.rearrange("p (t a i j) -> p a j i t", t=2, i=4, j=PACK)

        lo_bf = [tile("lo_bf%d" % g, [P, K_PASS], BF16) for g in range(PASSES)]
        lo_scales = tile("lo_scales", [P, PASSES * P], U8)
        lo_codes = tile("lo_codes", [P, PASSES * P], U32)
        hi_bf = tile("hi_bf", [P, PASSES * K_PASS], BF16)
        hi_codes = tile("hi_codes", [P, PASSES * P], U32)
        hi_scales = tile("hi_scales", [P, PASSES * P], U8)
        nat_bf = tile("nat_bf", [P, PASSES * 2 * K_PASS], BF16)
        up_codes = tile("up_codes", [P, PASSES * P], U32)
        up_scales = tile("up_scales", [P, PASSES * P], U8)
        nat_codes = tile("nat_codes", [P, PASSES * 2 * P], U32)
        nat_scales = tile("nat_scales", [P, PASSES * 2 * P], U8)
        nat_view = nat_bf[:].rearrange("p (u g t a i j) -> p g u a j i t", g=PASSES, t=2, u=2, i=4, j=PACK)

        for g in range(PASSES):
            nc.vector.tensor_copy(out=pair_view(lo_bf[g][:]), in_=raw_view(0, g)[:, 0])
            if g == 0:
                for t in range(2):
                    nc.scalar.activation(out=nat_view[:, g, 0, :, :, :, t], in_=raw_view(0, g)[:, 1, :, :, :, t], func=COPY)
            else:
                nc.scalar.copy(out=nat_view[:, g, 0], in_=raw_view(0, g)[:, 1])
            quantize(lo_codes[:, g * P : (g + 1) * P], lo_scales[:, g * P : (g + 1) * P], lo_bf[g][:])

        for g in range(PASSES):
            for t in range(2):
                col = (2 * g + t) * P
                quantize(nat_codes[:, col : col + HP], nat_scales[:, col : col + HP], nat_bf[:, 2 * col : 2 * col + 2 * P])

        pitch = T + SPARE
        h = tile("h", [P, (PACK + 1) * pitch], F32)
        slots = h[:].rearrange("p (s c) -> p s c", c=pitch)
        nc.vector.memset(slots[:, 0:1, T:], 0.0)
        nc.vector.memset(slots[:, 2:, T:], 0.0)
        place = (0, 4, 2, 3)

        def h_cols(w, c0=0, c1=T):
            return slice(place[w] * pitch + c0, place[w] * pitch + c1)

        def project(w, codes, scales, col, groups, bank):
            accs = [ps.tile([P, c1 - c0], F32, name="h_acc%d%d" % (w, i), tag="bank%d" % (bank + i))
                    for i, (c0, c1) in enumerate(groups)]
            for g in range(PASSES):
                for acc, (c0, c1) in zip(accs, groups):
                    mx(acc[:], codes[:, col(g) : col(g) + P], scales[:, col(g) : col(g) + P],
                       x_codes[g][:, c0:c1], x_planes[:, g, c0:c1], g == 0, g == PASSES - 1)
                    if g == PASSES - 1 and w == 0 and c0 == HALF:
                        nc.vector.tensor_scalar(out=h[:, h_cols(w, c0, c1)], in0=acc[:], scalar1=0.0,
                                                scalar2=None, op0=MAX)
                    elif g == PASSES - 1:
                        nc.scalar.activation(out=h[:, h_cols(w, c0, c1)], in_=acc[:], func=RELU)

        halves = [(0, HALF), (HALF, T)]
        project(0, lo_codes, lo_scales, lambda g: g * P, [(0, HALF), (HALF, FIRST), (FIRST, T)], 5)

        def gather(dst, w, d, v0, v1):
            width = T + SPARE if v1 - v0 == T else T
            start = h_cols(w).start
            nc.vector.tensor_copy(out=dst, in_=h[:, start : start + width].indirect(offs[d][:, v0 // 16 : v1 // 16]))

        def vmax(dst, one, other):
            nc.vector.tensor_tensor(out=dst, in0=one, in1=other, op=MAX)

        e = tile("e", [P, 2, 32, 32], BF16)[:, :, :, 0:16]
        gather(e[:, 0], 0, 0, 0, T)
        late = hi_raw[:].bitcast(BF16).rearrange("p (w r k v) -> p k w r v", w=2, k=2, v=16)[:, :, :, 0:32]
        two = late[:, 0]
        third = late[:, 1]
        for g in range(PASSES):
            nc.scalar.copy(out=pair_view(hi_bf[:, g * K_PASS : (g + 1) * K_PASS]), in_=raw_view(1, g)[:, 0])
            quantize(hi_codes[:, g * P : (g + 1) * P], hi_scales[:, g * P : (g + 1) * P],
                     hi_bf[:, g * K_PASS : (g + 1) * K_PASS])
            if g == 0:
                gather(two[:, 1], 0, 1, 0, T)
        for g in range(PASSES):
            nc.scalar.copy(out=nat_view[:, g, 1], in_=raw_view(1, g)[:, 1])
        vmax(two[:, 0], e[:, 0], two[:, 1])
        project(1, hi_codes, hi_scales, lambda g: g * P, halves, 2)
        quantize(up_codes[:], up_scales[:], nat_bf[:, PASSES * K_PASS :])
        nc.sync.dma_start(out=nat_codes[:].bitcast(I32).rearrange("p (k u c) -> p u k c", u=2, c=HP)[:, 1],
                          in_=up_codes[:].bitcast(I32).rearrange("p (k c) -> p k c", c=HP))
        nc.sync.dma_start(out=nat_scales[:].bitcast(I32).rearrange("p (k u c) -> p u k c", u=2, c=HP // 4)[:, 1],
                          in_=up_scales[:].bitcast(I32).rearrange("p (k c) -> p k c", c=HP // 4))
        wh_bf = tile("wh_bf", [P, (2 * N + T) * PACK], BF16, tag="nat_bf")
        nc.gpsimd.tensor_scalar(out=wh_bf[:, (N + T) * PACK :].rearrange("p (c t) -> p c t", t=PACK),
                                in0=w23_raw[:, 0].rearrange("p t c -> p c t"),
                                scalar1=1.0, scalar2=0.0, op0=mybir.AluOpType.mult, op1=ADD)
        nc.scalar.copy(out=wh_bf[:, 0 : N * PACK].rearrange("p (c i t) -> p c t i", i=4, t=PACK),
                       in_=w23_raw[:, 1].rearrange("p t (c i) -> p c t i", i=4))
        gather(third[:, 0], 0, 2, 0, T)
        both = tile("both", [P, 2, T], BF16)
        diff0 = tile("diff0", [P, T], F32)
        nc.gpsimd.tensor_tensor(out=diff0[:].rearrange("p (r v) -> p r v", v=16), in0=two[:, 0], in1=third[:, 0], op=SUB)
        nc.scalar.activation(out=diff0[:], in_=diff0[:], func=RELU)
        nc.gpsimd.tensor_tensor(out=both[:, 0].rearrange("p (r v) -> p r v", v=16),
                                in0=diff0[:].rearrange("p (r v) -> p r v", v=16), in1=third[:, 0], op=ADD)
        gather(two[:, 1], 1, 0, 0, T)
        gather(third[:, 1], 1, 1, 0, T)
        gather(e[:, 1], 1, 2, 0, T)
        vmax(both[:, 1].rearrange("p (r v) -> p r v", v=16), two[:, 1], third[:, 1])
        for w, groups in ((3, halves), (2, [(0, T)])):
            project(w, nat_codes, nat_scales, lambda g: (2 * g + w - 2) * P, groups, 4)
        zn = tile("zn", [P, 2, 4, P + GAP], BF16)[:, :, :, 0:P]
        second = tile("second", [P, 2, 4, P + GAP], BF16)[:, :, :, 0:P]
        gather(zn[:, 1], 3, 0, 0, T)
        zm1 = tile("zm1", [P, T], BF16, tag="x_codes0")
        vmax(zm1[:].rearrange("p (r v) -> p r v", v=16), both[:, 1].rearrange("p (r v) -> p r v", v=16), e[:, 1])
        zm = (both[:, 0], zm1[:])

        z01 = reuse.tile([P, 2, 3 * T], BF16, name="z01", offset=0, align_bytes=ALIGN)[:, :, 0:T]
        for w in range(2):
            for t in range(1 - w, 2):
                nc.sync.dma_start(out=slots[w * HP : (w + 1) * HP, t, 0:T],
                                  in_=h[t * HP : (t + 1) * HP, h_cols(w)])
        for w in range(2):
            for t in range(2):
                nc.sync.dma_start(out=z01[w * HP : (w + 1) * HP, t, :], in_=zm[w][t * HP : (t + 1) * HP])

        nc.scalar.copy(out=wh_bf[:, N * PACK : (N + T) * PACK].rearrange("p (c i t) -> p c t i", i=4, t=PACK),
                       in_=slots[:, 0:PACK, 0:T].rearrange("p t (c i) -> p c t i", i=4))
        z_bf = tile("z_bf", [P, T * PACK], BF16)[:]
        nc.scalar.copy(out=z_bf.rearrange("p (c i t) -> p c t i", i=4, t=PACK)[:, :, 0:2, :],
                       in_=z01.rearrange("p t (c i) -> p c t i", i=4))

        a2 = tile("a2", [P, 2, 3, P + GAP], BF16)[:, :, :, 0:P]
        gather(second[:, 1], 3, 1, 0, T)
        diff = tile("diff", [P, FIRST], F32)
        gain = slots[:, 1, 0:FIRST]
        nc.gpsimd.tensor_tensor(out=diff[:].rearrange("p (b v) -> p b v", v=P), in0=zn[:, 1, 1:4], in1=second[:, 1, 1:4], op=SUB)
        nc.scalar.activation(out=gain, in_=diff[:], func=RELU)
        nc.gpsimd.tensor_tensor(out=zn[:, 1, 1:4], in0=gain.rearrange("p (b v) -> p b v", v=P), in1=second[:, 1, 1:4], op=ADD)
        gather(a2[:, 1], 3, 2, LAST, T)
        gather(zn[:, 0], 2, 0, 0, T)
        gather(second[:, 0], 2, 1, 0, T)
        gather(a2[:, 0], 2, 2, LAST, T)
        five = zn.rearrange("p t b v -> p (t b) v")[:, 0:5]
        vmax(five, five, second.rearrange("p t b v -> p (t b) v")[:, 0:5])
        late_z = reuse.tile([P, 2, 2, T], BF16, name="late_z", offset=0, align_bytes=ALIGN)
        za = late_z[:, 0]
        for t in (1, 0):
            vmax(za[:, t, LAST:T].rearrange("p (b v) -> p b v", v=P), zn[:, t, 1:4], a2[:, t])
        for c0, c1 in ((HALF, T), (LAST, HALF)):
            nc.scalar.copy(
                out=z_bf[:, c0 * PACK : c1 * PACK].rearrange("p (c i t) -> p c t i", i=4, t=PACK)[:, :, 2:4, :],
                in_=za[:, :, c0:c1].rearrange("p t (c i) -> p c t i", i=4))
        wh_codes = tile("wh_codes", [P, 2 * N + T], U32)
        wh_scales = reuse.tile([P, 2 * N + T], U8, name="wh_scales", offset=8 * T, align_bytes=ALIGN)

        def quantize_wh(c0, c1):
            quantize(wh_codes[:, c0:c1], wh_scales[:, c0:c1], wh_bf[:, c0 * PACK : c1 * PACK])

        def weights(s, m):
            cols = slice((1 - s) * (N + T) + m * P, (1 - s) * (N + T) + (m + 1) * P)
            return wh_codes[:, cols], wh_scales[:, cols]

        groups = [(HALF, T), (LAST, HALF), (0, LAST)]
        banks = (0, 1, 2, 3, 6, 7)
        out_acc = {}
        z_codes = tile("z_codes", [P, T], U32)
        z_scales = tile("z_scales", [P, T], U8)

        def open_group(i):
            c0, c1 = groups[i]
            for m in range(N // P):
                acc = ps.tile([P, c1 - c0], F32, name="out_acc%d%d" % (i, m), tag="bank%d" % banks[2 * i + m])
                mx(acc[:], *weights(0, m), wh_codes[:, N + c0 : N + c1], wh_scales[:, N + c0 : N + c1], True, False)
                out_acc[i, m] = acc

        def quantize_z(i):
            c0, c1 = groups[i]
            quantize(z_codes[:, c0:c1], z_scales[:, c0:c1], z_bf[:, c0 * PACK : c1 * PACK])

        def close_group(i, m):
            c0, c1 = groups[i]
            mx(out_acc[i, m][:], *weights(1, m), z_codes[:, c0:c1], z_scales[:, c0:c1], False, True)

        b2 = za.rearrange("p b (t v) -> p t b v", t=2)[:, :, :, 0:BLOCK]
        quantize_wh(T, 2 * T)
        quantize_wh(0, N)
        open_group(0)
        gather(b2[:, 0], 2, 2, 0, LAST)
        quantize_z(0)
        res = tile("first_out", [P, N // P, HALF], F32)
        for m in range(N // P):
            close_group(0, m)
            nc.scalar.activation(out=res[:, m, :], in_=out_acc[0, m][:], func=RELU)
            nc.sync.dma_start(out=out[m * P : (m + 1) * P, HALF:T], in_=res[:, m, :])
        gather(b2[:, 1], 3, 2, 0, LAST)
        quantize_wh(N, T)
        open_group(1)
        open_group(2)
        vmax(z_bf[:, 0 : LAST * PACK].rearrange("p (b v t) -> p b v t", b=2, t=PACK)[:, :, :, 2:4],
             zn[:, :, 0].rearrange("p t (b v) -> p b v t", b=2), b2.rearrange("p t b v -> p b v t"))
        quantize_z(1)
        quantize_z(2)
        res = tile("second_out", [P, N // P, LAST], F32)
        for m in range(N // P):
            close_group(1, m)
            nc.scalar.activation(out=res[:, m, :], in_=out_acc[1, m][:], func=RELU)
        nc.sync.dma_start(out=out[:, LAST:HALF].rearrange("(m p) v -> p m v", p=P), in_=res[:])
        res = tile("last_out", [P, N // P, LAST], F32)
        for m in range(N // P):
            close_group(2, m)
        nc.scalar.activation(out=res[:, 0, :], in_=out_acc[2, 0][:], func=RELU)
        nc.vector.tensor_scalar(out=res[:, 1, :], in0=out_acc[2, 1][:], scalar1=0.0, scalar2=None, op0=MAX)
        nc.sync.dma_start(out=out[:, 0:LAST].rearrange("(m p) v -> p m v", p=P), in_=res[:])
